import numpy as np, ml_dtypes
CORES = [40,41,42,43,44,45,46,47]
N = 8
import mx_ref
BF = ml_dtypes.bfloat16
def gentries(a):
    return np.ascontiguousarray(a.reshape(8, 16, -1).transpose(0, 2, 1)).reshape(8, -1)
def gtable(e):
    e = np.asarray(e); return np.ascontiguousarray(e.reshape(8, -1, 16).transpose(0, 2, 1)).reshape(128, -1).astype(np.int32)
def gcols(t, e):
    v = np.concatenate([t.reshape(8, 16, -1, 4), np.zeros((8, 16, 1, 4), BF)], axis=2)
    return np.ascontiguousarray(np.stack([v[g][:, e[g]] for g in range(8)])).reshape(128, -1)
def tile(rs):
    return np.stack(rs, axis=2).reshape(128, -1).astype(BF)
def pick(q, e):
    c = np.concatenate([q[0].reshape(128, -1, 4), np.zeros((128, 1, 4), np.uint8)], axis=1); s = np.concatenate([q[1], np.ones((16, 1), np.uint8)], axis=1)
    return (np.ascontiguousarray(c[:, e].reshape(128, -1)), np.ascontiguousarray(s[:, e]))
def join(*qs):
    return (np.concatenate([q[0] for q in qs], axis=1), np.concatenate([q[1] for q in qs], axis=1))
def put(q, e, v):
    c, s = q[0].reshape(128, -1, 4).copy(), q[1].copy(); c[:, e] = v[0].reshape(128, -1, 4); s[:, e] = v[1]
    return (c.reshape(128, -1), s)
def pk(c, s):
    return (np.ascontiguousarray(c), mx_ref.live(s))
def emit(q):
    return q[0], q[1]
def packed(v, rng):
    q = [mx_ref.quantize(np.ascontiguousarray(v[r])) for r in range(N)]
    return np.stack([a for a, b in q]), np.stack([mx_ref.plane(b, rng) for a, b in q])
def values_of_codes():
    e, c = np.zeros((128, 128, 4), np.float32), np.zeros((128, 2, 4), np.uint8)
    e[np.arange(128), np.arange(128), 0] = 1
    c[:127, :, 0] = np.arange(256).reshape(2, 128).T[:127]
    return mx_ref.matmul(mx_ref.quantize(e.reshape(128, 512).astype(BF)), (c.reshape(128, 8), np.full((16, 2), 127, np.uint8))).T.reshape(-1).astype(np.float64)
CODE_VALUE, SCALE_VALUE = values_of_codes(), 2.0 ** (np.arange(256) - 127.0)
def decode(q):
    return (CODE_VALUE[q[0]].reshape(16, 8, -1, 4) * SCALE_VALUE[q[1]][:, None, :, None] + 0.0).reshape(128, -1).astype(np.float32)
def f(rng, *shape):
    return mx_ref.flush((rng.standard_normal(shape, dtype=np.float32) * np.exp2(rng.integers(-2, 3, shape[:-1] + (1,)))).astype(BF))
def wide(rng, *shape, cols=0):
    v = rng.standard_normal(shape, dtype=np.float32) * np.exp2(rng.integers(-12, 13, shape)).astype(np.float32)
    if cols: v *= np.repeat(np.exp2(rng.integers(-cols, cols + 1, shape[:-2] + (1, shape[-1] // 4))) * (rng.random(shape[:-2] + (1, shape[-1] // 4)) > 0.0625), 4, axis=-1).astype(np.float32)
    return mx_ref.flush(v.astype(BF))
C, GW, R, SWEEPS = 320, 64, 3, 6
JUMP = [0, 1, 4]
def big(v):
    v = v.astype(np.float32)
    v[np.abs(v) < np.float32(2.0 ** -16)] = 0
    return v.astype(BF)
def numbers_of(rng):
    return {"x": big(f(rng, N, 128, 4 * C)), "u": np.array(f(rng, N, 128, 512)), "v": np.array(f(rng, N, 128, 512))}
def weights(rng, still=[]):
    w = big(f(rng, N, 128, 2048)).reshape(N, 8, 16, 4, 8, 16, 4)
    for i in still:
        w[:, :, i] = 0
        w[:, :, :, :, :, i] = 0
    c, p = packed(w.reshape(N, 128, 2048), rng)
    return {"wc": c, "ws": p}
def ltable(a):
    return gtable(a.transpose(1, 0, 2).reshape(8, 3 * C))
def drawn(rng):
    a = np.zeros((3, 8, C), np.int64)
    for g in range(8):
        o = rng.permutation(C)
        a[0, g, o[::2]] = o[1::2]
        a[0, g, o[1::2]] = o[::2]
        for k in (1, 2):
            if g & JUMP[k] == 0:
                o = rng.permutation(C)
                a[k, g] = o
                a[k, g ^ JUMP[k], o] = np.arange(C)
    return a
def links(rng):
    return np.stack([ltable(drawn(rng)) for r in range(N)])
def setup_inputs(rng):
    return {**numbers_of(rng), "lk": links(rng), **weights(rng)}
def setup_inputs_ties(rng):
    d = numbers_of(rng)
    x = d["x"].reshape(N, 8, 16, C, 4)
    x[:, :, 0] = 0
    x[:, :, 0, :, 0] = rng.integers(0, 4, (N, 8, C)).astype(np.float32).astype(BF)
    u = d["u"].reshape(N, 128, 128, 4)
    u[:, :, ::16] = 0
    o = rng.permutation(N)
    for r in range(N):
        for h in range(0, 128, 16): u[r, h, h, 0] = 0.0 if r == o[0] else -1.0 if r == o[1] else 1.0
    return {"x": x.reshape(N, 128, 4 * C), "u": u.reshape(N, 128, 512), "v": d["v"], "lk": links(rng), **weights(rng, [0])}
def setup_inputs_near(rng):
    d = numbers_of(rng)
    x = d["x"].astype(np.float32).reshape(N, 8, 16, C, 4)
    x[:, :, 0] = 0
    x[:, :, 8:] = 0
    x[:, :, 0, :, 0] = 1
    s = rng.integers(0, 16, (N, 8, C))
    x[:, :, 8] = ((s[:, :, :, None] >> np.arange(4)) & 1) * np.exp2(np.arange(4) - 21.0)
    x[:, :, 11, :, 0] = 2.0 ** -10
    u = d["u"].reshape(N, 128, 128, 4)
    u[:, :, ::16] = 0
    o = rng.permutation(N) % 4
    for r in range(N):
        far = rng.permutation(8)
        if o[r] == 0: x[r, :, 0, :, 0] = 7
        if o[r] == 1: x[r, :, 0, :, 0] = -1
        if o[r] < 2:
            for i in range(4): x[r, far[i], 0, rng.integers(C), 0] = (-1.5 if i == 0 else 1.5) * 2.0 ** 29
        if o[r] == 3:
            x[r, :, 8:] = 0
            x[r, :, 10, :, 0] = (8 + rng.integers(0, 8, (8, C))) * 2.0 ** -33
        k = 1.0 if o[r] == 0 else 2.0 ** -30
        for g in range(8):
            h = 16 * g
            if o[r] < 2:
                u[r, h, h, 0] = k
                u[r, h + 11, h, 0] = k
            if o[r] == 2 and g == far[0]: u[r, h, h, 0] = 1.0
            if o[r] == 2 and g == far[1]: u[r, h, h, 0] = -1.0
            if o[r] < 3: u[r, h + 8, h] = k
            else: u[r, h + 10, h, 0] = k * 1.125 if g >= 4 else k
    return {"x": x.reshape(N, 128, 4 * C).astype(BF), "u": u.reshape(N, 128, 512), "v": d["v"], "lk": links(rng), **weights(rng, [0, 8, 9, 10, 11, 12, 13, 14, 15])}
def setup_inputs_cubes(rng):
    d = numbers_of(rng)
    x = d["x"].reshape(N, 8, 16, C, 4)
    x[:, :, 0] = 0
    low = (1.125 + 0.25 * rng.integers(0, 4, (N, 8, 8, C, 4))) * np.exp2(10.0 - rng.integers(8, 15, (N, 8, 8, C, 4)))
    x[:, :, 8:] = (low * rng.choice([-1.0, 1.0], (N, 8, 8, C, 4))).astype(np.float32).astype(BF)
    x[:, :, 8, :, 0] = 2016.0
    u = d["u"].reshape(N, 128, 128, 4)
    u[:, :, ::16] = 0
    p, e = [], rng.permutation(N)
    for r in range(N):
        o = rng.permutation(C) if e[r] % 2 else np.arange(C)
        k = np.zeros(C, np.float32)
        k[o] = np.repeat(rng.integers(-7, 8, C // 2), 2)
        x[r, :, 0, :, 0] = k.astype(BF)
        a = np.tile(np.arange(C), (3, 8, 1))
        a[0][:, o] = o[np.arange(C) ^ 1]
        p.append(ltable(a))
        for h in range(0, 128, 16): u[r, h, h, 0] = -1.0 if e[r] == 0 else 1.0
    w = big(f(rng, N, 128, 2048)).reshape(N, 8, 16, 4, 8, 16, 4)
    w[:, :, 0] = 0
    w[:, :, 8, :, :, :, 0] = 0
    w[:, :, :, :, :, 0] = 0
    w[:, :, :, :, :, 8:] = 0
    for g in range(8): w[:, g, 8, 0, g, 8, 0] = -1.0
    c, s = packed(w.reshape(N, 128, 2048), rng)
    return {"x": x.reshape(N, 128, 4 * C), "u": u.reshape(N, 128, 512), "v": d["v"], "lk": np.stack(p), "wc": c, "ws": s}
def setup_inputs_ends(rng):
    d = numbers_of(rng)
    o = rng.permutation(N) % 4
    a, b = np.flatnonzero(o < 2)[:2]
    o[[a + 1, b]] = o[[b, a + 1]]
    sg = rng.choice([-1.0, 1.0], N)
    x = np.ones((N, 8, 16, C, 4))
    u = d["u"].astype(np.float32).reshape(N, 8, 16, 8, 16, 4)
    u[:, :, :, :, 0] = 0
    v = rng.choice([-1.0, 1.0], (N, 128, 512))
    w = np.zeros((N, 128, 4, 128, 4), np.float32)
    i, p = np.arange(128), []
    for r in range(N):
        large = o[r] < 2
        size = 2.0 ** 30 if large else 2.0 ** -30
        h = rng.permutation(8)
        x[r, h[4:]] = rng.choice([1.0, 0.875, 0.75] if large else [1.0, 1.125, 1.25], (4, 1, C, 1))
        x[r] *= sg[r] * size
        v[r] *= size
        k = size * sg[r] * (1.0 if o[r] % 2 == 0 else -1.0)
        for g in range(8):
            for c in (h[:4] if g in h[:4] else h): u[r, c, :, g, 0] = k
        for b in range(4): w[r, i, b, i, b] = sg[r] * sg[r - 1] * (-2.0 if large else 2.0)
        a = drawn(rng)
        if large:
            a[:2] = C - 1 - np.arange(C)
            a[2] = np.arange(C)
        p.append(ltable(a))
    c, s = packed(w.reshape(N, 128, 2048).astype(BF), rng)
    return {"x": x.reshape(N, 128, 4 * C).astype(np.float32).astype(BF), "u": u.reshape(N, 128, 512).astype(BF), "v": v.astype(np.float32).astype(BF), "lk": np.stack(p), "wc": c, "ws": s}
def setup_inputs_spread(rng):
    d = setup_inputs(rng)
    d["x"] = big(wide(rng, N, 128, 4 * C, cols=6))
    return d
def check_inputs(d):
    b = []
    for k in ("x", "u", "v"):
        a = np.abs(d[k].astype(np.float32))
        if not (np.isfinite(a).all() and ((a == 0) | (a >= 2.0 ** -30) & (a <= 2.0 ** 30)).all()): b.append("a value of " + k)
    none, least, most = [emit(mx_ref.quantize(np.full((128, 16), k, np.float32).astype(BF)))[1][0, 0] for k in (0.0, 2.0 ** -16, 2.0 ** 5)]
    for r in range(N):
        e = gentries(d["lk"][r])
        if not ((e >= 0) & (e < C)).all(): b.append("an entry of lk")
        else:
            n = other_ends(d["lk"][r])
            if (np.take_along_axis(n, n, axis=1) != np.arange(8 * C)).any(): b.append("a link of lk isn't the same from both ends")
            if (n == np.arange(8 * C)).any(): b.append("a link of lk from a node to itself")
        if ((d["wc"][r] == 0x7F) | (d["wc"][r] == 0xFF)).any(): b.append("wc: a code that is no number")
        s = mx_ref.live(d["ws"][r])
        if ((s != none) & ((s < least) | (s > most))).any(): b.append("ws: a scale out of range")
    return b
def other_ends(a):
    e = gentries(a).reshape(8, 3, C).astype(np.int64)
    return np.stack([(e[:, k] + C * (np.arange(8) ^ JUMP[k])[:, None]).reshape(-1) for k in range(3)])
def parts(t):
    return t.reshape(8, 16, -1, 4).transpose(0, 2, 1, 3).reshape(-1, 16, 4)
def whole(p):
    return np.ascontiguousarray(p.reshape(8, -1, 16, 4).transpose(0, 2, 1, 3)).reshape(128, -1)
def reference(x, u, v, lk, wc, ws):
    qu = [mx_ref.quantize(u[r]) for r in range(N)]
    lay = [pk(wc[r], ws[r]) for r in range(N)]
    ends = [other_ends(lk[r]) for r in range(N)]
    now = [x[r] for r in range(N)]
    node = np.arange(8 * C)
    away, mark = [None] * N, [np.zeros((3, 8 * C), bool) for r in range(N)]
    route = [None] * N
    for t in range(R):
        sent, blend, gate = [], [], []
        for r in range(N):
            q, n = mx_ref.quantize(now[r]), ends[r]
            s = mx_ref.matmul(qu[r], q)[::16] + np.float32(0.0)
            l = np.argsort(s, axis=1, kind="stable")[:, :GW]
            slot = np.full((8, C), -1)
            np.put_along_axis(slot, l, np.tile(np.arange(GW), (8, 1)), axis=1)
            slot, s = slot.reshape(-1), s.reshape(-1)
            a, m = away[r], mark[r]
            if t == 0: a = (s[n] < s) | (s[n] == s) & (n < node)
            for i in range(SWEEPS):
                sink = ~a.any(axis=0) & (slot < 0)
                turn = sink & (~m | m.all(axis=0))
                came = np.take_along_axis(turn, n, axis=1)
                a = (a | turn) & ~came
                m = (m & ~sink) | came
            away[r], mark[r] = a, m
            k = np.argmin(np.where(a, s[n], np.float32(np.inf)), axis=0)
            to = np.where((slot < 0) & a.any(axis=0), n[k, node], node)
            e = to[to]
            e = e[e]
            own = decode(q)
            p = parts(own)
            blend.append(((p[to] + p[e]) * np.float32(0.5)).astype(BF))
            sent.append(mx_ref.quantize(gcols(own.astype(BF), l)))
            gate.append(slot)
            route[r] = e
        for r in range(N):
            h = parts(tile([mx_ref.matmul(pick(lay[r], np.arange(128 * b, 128 * b + 128)), sent[r - 1]) * np.float32(0.015625) for b in range(4)]))
            z, e, k = blend[r], route[r], gate[r][route[r]]
            w = k >= 0
            z[w] = (z[w].astype(np.float32) + h[GW * (e[w] // C) + k[w]].astype(np.float32)).astype(BF)
            now[r] = whole(z)
    y, nd = np.zeros((N, 128, C), np.float32), np.zeros((N, 8, 2 * C), np.float32)
    oc, osc = np.zeros((N, 128, 4 * C), np.uint8), np.zeros((N, 16, C), np.uint8)
    for r in range(N):
        q = mx_ref.quantize(now[r])
        y[r] = mx_ref.matmul(mx_ref.quantize(v[r]), q)
        nd[r, :, :C] = route[r].reshape(8, C)
        a, m = away[r].astype(np.int64), mark[r].astype(np.int64)
        nd[r, :, C:] = (a[0] + 2 * a[1] + 4 * a[2] + 8 * m[0] + 16 * m[1] + 32 * m[2]).reshape(8, C)
        oc[r], osc[r] = emit(q)
    return {"y": y, "nd": nd, "oc": oc, "osc": osc}

@@ -1,0 +1,570 @@
+from concourse.bass import DstId, RemoteDMATransfer
+from concourse.mybir import dt, AluOpType as A, ActivationFunctionType as F
+
+C, GW, R, SWEEPS = 320, 64, 3, 6
+BF, F32, I32, U16, X4, U8 = "bfloat16", "float32", "int32", "uint16", "float8_e4m3fn_x4", "uint8"
+SPLIT = 14
+
+SCRATCH = {}
+
+
+def _s(n, w, d):
+    SCRATCH[n] = ("sbuf", [128, w], d)
+
+
+def _q(n, w):
+    _s(n + "c", w, X4)
+    _s(n + "s", w, U8)
+
+
+for _n, _w in (("xt", 1280), ("ut", 512), ("vt", 512), ("sga", 320), ("sgb", 320), ("gp", 1280), ("pp", 1280), ("st", 1280),
+               ("pub", 320), ("kt", 1280), ("eqe", 320), ("eqo", 320), ("et", 512), ("zero", 512), ("foa", 640), ("fob", 640),
+               ("f4a", 2560), ("f4b", 2560), ("ho", 320), ("h4", 1280), ("zd", 1280), ("zz", 1280), ("ident", 128),
+               ("ones", 128), ("ra", 128), ("rb", 128), ("pe", 128), ("po", 128), ("rel0", 128), ("rel1", 128), ("rel4", 128),
+               ("om", 128 * 23), ("ce", 2048), ("flg", 1280)):
+    _s(_n, _w, BF)
+for _i in range(6):
+    _s("rt%d" % _i, 1280, BF)
+CONSTS = ["cm", "cmw", "ci1", "ci2", "cb", "cbw", "cpw", "cs", "ck", "ckg", "cn2", "cr", "cr5"]
+OM = {_n: 128 * _i for _i, _n in enumerate([_x + _y for _x in ("om", "on", "w", "u") for _y in "012go"] + ["tm0", "tm1", "tm2"])}
+LOC = {"eb": ("qk", 0, 512)}
+for _i, _n in enumerate(CONSTS):
+    _s(_n, 512, BF)
+    LOC["q" + _n] = ("qk", 512 + 128 * _i, 128)
+_q("qk", 512 + 128 * len(CONSTS))
+for _i, _n in enumerate(("gq0", "gq1", "pq0", "pq1", "ra_", "rb_", "sq", "kq")):
+    LOC[_n] = ("qf", 320 * _i, 320)
+_q("qf", 320 * 8)
+for _i in range(R):
+    LOC["qe%d" % _i] = ("qe", 128 * _i, 128)
+_q("qe", 128 * R)
+for _n, _w in (("ns", 960), ("tb", 320), ("tc", 320), ("mk", 320), ("sc", 320), ("srt", 320), ("dsrc", 640), ("ds4", 2560),
+               ("iot", 2560), ("num", 2560), ("mask", 320), ("sc0", 320), ("ioj", 320), ("lwd", 60), ("kz", 60), ("kd", 60),
+               ("dl", 20), ("dl2", 20), ("nat", 20), ("cols", 32), ("kc0", 448), ("kct", 448), ("g1", 320), ("g2", 320),
+               ("ndr", 640), ("ysb", 320), ("lrow", 320)):
+    _s(_n, _w, F32)
+for _n, _w in (("lki", 60), ("ki", 20), ("kb", 60), ("kcst", 60), ("ip", 1), ("ib", 8), ("inat", 20), ("imask", 320), ("iu", 40)):
+    _s(_n, _w, I32)
+for _n, _w in (("lk16", 60), ("rw", 20), ("lg", 4), ("dl16", 20), ("c1", 20), ("c2", 20), ("e16", 20), ("hl", 20), ("ul", 40)):
+    _s(_n, _w, U16)
+for _n, _w in (("qu", 128), ("ua", 640), ("qv", 128), ("qw", 512), ("qx", 320)):
+    _q(_n, _w)
+for _i in range(R):
+    _q("aq%d" % _i, 192)
+for _i in range(8):
+    SCRATCH["ps%d" % _i] = ("psum", [128, 512], F32)
+
+SEMAPHORES = ["sv", "ss", "st_", "sg_", "ldx", "ldu", "ldv", "ldw", "ldl", "ndo", "yo", "oco"]
+for _i in range(R):
+    SEMAPHORES += ["fd%d" % _i, "dd%d" % _i, "hd%d" % _i, "arr%d" % _i, "snt%d" % _i]
+
+
+def rank_program(g, core, T, topo):
+    rank = T.rank_of(core)
+    if rank is None:
+        return
+    nxt = T.cores[(rank + 1) % len(T.cores)]
+    ENG = {"v": g.vector, "s": g.scalar, "t": g.tensor, "g": g, "y": g.sync}
+    CS = {"v": "sv", "s": "ss", "t": "st_", "g": "sg_"}
+    tot, know, lastw, readers = {}, {q: {} for q in ENG}, {}, {}
+    dmasem = set()
+
+    def settle(q, toks):
+        want = {}
+        for sem, val, clk, e in toks:
+            if sem in dmasem:
+                val = tot[sem]
+            if sem not in want or want[sem][0] < val:
+                want[sem] = (val, clk)
+        k = know[q]
+        for sem in sorted(want):
+            val, clk = want[sem]
+            if k.get(sem, 0) < val:
+                ENG[q].wait_ge(T.sem[sem], val)
+                for a, b in clk.items():
+                    if k.get(a, 0) < b:
+                        k[a] = b
+                k[sem] = val
+
+    def deps(q, reads, writes, dma):
+        toks = []
+        for r in reads:
+            toks += lastw.get(r, [])
+            if r[:2] == "ps" and r[2:].isdigit():
+                toks += [x for x in readers.get(r, []) if x[3] != q]
+        for w in writes:
+            toks += [x for x in lastw.get(w, []) if dma or x[3] != q or q != "t"]
+            toks += readers.get(w, [])
+        return toks
+
+    def done(tok, reads, writes):
+        for r in reads:
+            if r not in writes:
+                readers.setdefault(r, []).append(tok)
+        for w in writes:
+            lastw[w] = [tok]
+            readers[w] = []
+
+    def op(q, reads, writes, fn):
+        reads, writes = reads.split(), writes.split()
+        sem = CS[q]
+        pool = [(sem, tot[sem], {}, q)] if q == "g" and sem in tot else []
+        settle(q, deps(q, reads, writes, False) + pool)
+        fn(ENG[q]).then_inc(T.sem[sem], 1)
+        tot[sem] = tot.get(sem, 0) + 1
+        clk = dict(know[q])
+        clk[sem] = tot[sem]
+        done((sem, tot[sem], clk, q), reads, writes)
+
+    def dma(moves, sem, reads, writes):
+        reads, writes = reads.split(), writes.split()
+        dmasem.add(sem)
+        toks = deps("", reads, writes, True)
+        qs = []
+        for q, o, i in moves:
+            if q not in qs:
+                qs.append(q)
+                settle(q, toks)
+            ENG[q].dma_start(o, i).then_inc(T.sem[sem], 16)
+            tot[sem] = tot.get(sem, 0) + 16
+        clk = {}
+        for q in qs:
+            for a, b in know[q].items():
+                clk[a] = max(clk.get(a, 0), b)
+        clk[sem] = tot[sem]
+        done((sem, tot[sem], clk, "dma"), reads, writes)
+
+    def ts(o, i, s1, o1, reads, writes, s2=None, o2=None, q="v"):
+        if o2 is None:
+            op(q, reads, writes, lambda e: e.tensor_scalar(o, i, s1, None, o1))
+        else:
+            op(q, reads, writes, lambda e: e.tensor_scalar(o, i, s1, s2, o1, o2))
+
+    def tt(o, a, b, f, reads, writes):
+        op("v", reads, writes, lambda e: e.tensor_tensor(o, a, b, f))
+
+    def cp(o, i, reads, writes):
+        op("v", reads, writes, lambda e: e.tensor_copy(o, i))
+
+    def act(o, i, reads, writes, f=F.Copy, **kw):
+        op("s", reads, writes, lambda e: e.activation(o, i, f, **kw))
+
+    def fill(o, v, writes):
+        op("v", "", writes, lambda e: e.memset(o, v))
+
+    def quant(n, tile, tkeys, k=None, a=0, b=None):
+        n2, o, w = LOC.get(n, (n, 0, None))
+        c, s = T[n2 + "c"], T[n2 + "s"]
+        b = b if b is not None else w or c.shape[1]
+        a, b = a + o, b + o
+        op("v", tkeys, k or n, lambda e: e.quantize_mx(c[:, a:b], s[:, a:b], tile))
+
+    def mm(bank, l, r, start, stop, la=0, ra=0, n=C, lk=None, rk=None):
+        p = T["ps%d" % bank]
+        l2, lo, _w = LOC.get(l, (l, 0, 0))
+        r2, ro, _w = LOC.get(r, (r, 0, 0))
+        x, y = la + lo, ra + ro
+        op("t", (lk or l) + " " + (rk or r), "ps%d" % bank, lambda e: e.matmul_mx(
+            p[:, 0:n], T[l2 + "c"][:, x:x + 128], T[l2 + "s"][:, x:x + 128], T[r2 + "c"][:, y:y + n], T[r2 + "s"][:, y:y + n], start, stop))
+
+    def ps(i, a=0, b=C):
+        return T["ps%d" % i][:, a:b]
+
+    def om(n, a=0, st=1):
+        return T.om[:, OM[n] + a:OM[n] + 128:st]
+
+    dma([("y", T.xt[:], T.x[:])], "ldx", "", "xt")
+    dma([("s", T.ut[:], T.u[:])], "ldu", "", "ut")
+    dma([("s", T.lki[:], T.lk[:])], "ldl", "", "lki")
+    dma([("y", T.qwc[:].bitcast(dt.uint8), T.wc[:]), ("y", T.qws[:], T.ws[:])], "ldw", "", "qw")
+    dma([("s", T.vt[:], T.v[:])], "ldv", "", "vt")
+
+    def iota(o, pat, base, ch, w, fl=False):
+        if fl:
+            op("g", "", w, lambda e: e.iota(o, pat, base, ch, allow_small_or_imprecise_dtypes=True))
+        else:
+            op("g", "", w, lambda e: e.iota(o, pat, base, ch))
+
+    def asel(o, i, pat, cmp, base, ch, r, w):
+        op("g", r, w, lambda e: e.affine_select(o, i, pat, cmp, 0.0, base, ch))
+
+    fill(T.ones[:], 1.0, "ones")
+    for k, pat in enumerate(([[16, 8]], [[32, 4], [-16, 2]], [[-64, 2], [16, 4]], [[32, 4], [0, 2]], [[32, 4], [0, 2]])):
+        iota(T.iu[:, 8 * k:8 * k + 8], pat, (0, 16, 64, 0, 16)[k], 0, "iu%d" % k)
+    iota(T.ip[:], [[0, 1]], 0, 1, "ip")
+    iota(T.imask[:], [[1, C]], 128, -1, "imask")
+    iota(T.inat[:], [[16, 20]], 0, 0, "inat")
+    iota(T.ioj[:], [[1, C]], 0, 0, "ioj", True)
+    cp(T.ul[:], T.iu[:], "iu0 iu1 iu2 iu3 iu4", "ul")
+    quant("qu", T.ut[:], "ut")
+    op("v", "qu ul", "uac", lambda e: e.tensor_copy(T.uac[:].bitcast(dt.uint32), T.quc[:].bitcast(dt.uint32).indirect(T.ul[:, 0:40])))
+    op("s", "qu ul", "uas", lambda e: e.activation(T.uas[:], T.qus[:].indirect(T.ul[:, 0:40]), F.Copy))
+    cl = {}
+
+    def col(name):
+        cl.setdefault(name, len(cl))
+        return T.cols[:, cl[name]:cl[name] + 1]
+
+    for i, (sh, an) in enumerate(((4, 1), (5, 1), (6, 1), (0, 15))):
+        op("v", "ip", "ib%d" % i, lambda e: e.tensor_scalar(T.ib[:, i:i + 1], T.ip[:], sh, an, A.logical_shift_right, A.bitwise_and))
+        cp(col("b%d" % i), T.ib[:, i:i + 1], "ib%d" % i, "c_b%d" % i)
+    ts(col("a640"), col("b2"), 2.0, A.mult, "c_b2 c_b0", "c_a2", col("b0"), A.add)
+    ts(col("off"), col("b0"), 160.0, A.mult, "c_b0", "c_off")
+    ts(col("t63"), col("b0"), -160.0, A.mult, "c_b0", "c_t63", 63.5, A.add)
+    ts(col("s1"), col("a640"), 320.0, A.mult, "c_a2 c_off", "c_s1", col("off"), A.add)
+    ts(col("s2"), col("a640"), 320.0, A.mult, "c_a2", "c_s2", 64.0, A.add)
+    ts(col("m1"), col("b0"), -1280.0, A.mult, "c_b0", "c_m1", 640.0, A.add)
+    ts(col("m2"), col("b2"), -2560.0, A.mult, "c_b2", "c_m2", 1280.0, A.add)
+    ts(col("cl"), col("b1"), 640.0, A.mult, "c_b1", "c_cl")
+    ts(col("oa"), col("a640"), 640.0, A.mult, "c_a2 c_b3", "c_oa", col("b3"), A.add)
+    fill(T.kc0[:], 0.0, "kc0")
+    VEC = {"g0": {0: -3, 3: -3, 4: 3}, "g1": {5: -3, 6: -3, 7: 3}, "g2": {8: -3, 9: -3, 10: 3}, "x0": {0: 5, 3: 3, 4: -4, 11: 1},
+           "x1": {1: 5, 3: 3, 4: -4, 12: 1}, "x2": {2: 5, 3: 3, 4: -4, 13: 1}, "i0": {0: 1}, "kv": {11: 1, 12: 2, 13: 4, 3: 8},
+           "bb": {11: 1, 12: 2, 13: 4}, "s0": {11: 1}, "s1": {12: 1}, "s2": {13: 1}, "lo": {11: -99, 12: -99, 13: -99}, "hi": {11: 99, 12: 99, 13: 99}}
+    vi = {n: i for i, n in enumerate(VEC)}
+    fill(T.kc0[:, 32 * vi["hi"]:32 * vi["hi"] + 32], 1.0, "kc0")
+    for n, d in VEC.items():
+        o = 32 * vi[n]
+        for r, w in d.items():
+            fill(T.kc0[:, o + r:o + 32:16], float(w), "kc0")
+    op("v", "kc0", "kct", lambda e: e.transpose(T.kct[:], T.kc0[:]))
+
+    def vec(n):
+        return T.kct[:, 32 * vi[n]:32 * vi[n] + 1]
+
+    for n, p1, b1, p2, b2 in (("rel0", [[-16, 8], [0, 16]], 0, [[16, 8], [0, 16]], 15),
+                              ("rel1", [[-32, 4], [16, 2], [0, 16]], -16, [[32, 4], [-16, 2], [0, 16]], 31),
+                              ("rel4", [[64, 2], [-16, 4], [0, 16]], -64, [[-64, 2], [16, 4], [0, 16]], 79)):
+        asel(T.ra[:], T.ones[:], p1, A.is_ge, b1, 1, "ones", "ra")
+        asel(T[n][:], T.ra[:], p2, A.is_ge, b2, -1, "ra", n)
+    asel(T.ra[:], T.ones[:], [[-32, 4], [0, 32]], A.is_ge, 0, 1, "ones", "ra")
+    asel(T.rb[:], T.ra[:], [[32, 4], [0, 32]], A.is_ge, 31, -1, "ra", "rb")
+    asel(T.pe[:], T.rb[:], [[0, 4], [1, 2], [0, 16]], A.is_equal, 0, 0, "rb", "pe")
+    asel(T.po[:], T.rb[:], [[0, 4], [1, 2], [0, 16]], A.not_equal, 0, 0, "rb", "po")
+    asel(T.ident[:], T.ones[:], [[-1, 128]], A.is_equal, 0, 1, "ones", "ident")
+
+    for n in ("cr5", "ce", "ci2", "ck", "ckg", "cn2", "cs", "cb", "cbw", "cpw"):
+        fill(T[n][:], 0.0, n)
+    act(T.cr[:, 0::4], T.pe[:], "pe", "cr_0")
+    act(T.cr[:, 1::4], T.pe[:], "pe", "cr_1")
+    act(T.cr[:, 2::4], T.po[:], "po", "cr_2", scale=0.5)
+    act(T.cr[:, 3::4], T.po[:], "po", "cr_3", scale=0.5)
+    act(T.cr5[:, 0::4], T.pe[:], "pe", "cr5")
+    act(T.cr5[:, 1::4], T.po[:], "po cr5", "cr5_")
+    quant("qcr", T.cr[:], "cr_0 cr_1 cr_2 cr_3")
+    quant("qcr5", T.cr5[:], "cr5 cr5_")
+    op("v", "imask", "imask", lambda e: e.tensor_scalar(T.imask[:], T.imask[:], 15, None, A.bitwise_and))
+    ts(T.mask[:], T.imask[:], 0.0, A.is_equal, "imask", "mask")
+    fill(T.sc0[:], 1.0, "sc0")
+    fill(T.sc0[:, 0:C:16], 0.0, "sc0")
+    cp(T.lk16[:], T.lki[:], "lki", "lk16")
+    for z in ("gp", "pp", "st", "kt", "flg", "rt5", "et", "zero", "ho"):
+        fill(T[z][:], 0.0, z)
+    for b in range(4):
+        act(T.ce[:, 512 * b + b:512 * b + 512:4], T.ident[:], "ident ce", "ce_%d" % b, scale=0.5)
+    quant("eb", T.ce[:], "ce ce_0 ce_1 ce_2 ce_3")
+    Z = {11: 0, 12: 0, 13: 0, 14: 0, 15: 0}
+    for n, base, special in (("om0", -1.0, {**Z, 0: -4, 11: 1}), ("om1", -1.0, {**Z, 1: -4, 5: -4, 12: 1}),
+                             ("om2", -1.0, {**Z, 2: -4, 8: -4, 13: 1}), ("omg", -8.0, Z), ("omo", 4.0, {**Z, 4: 3, 7: 3, 10: 3}),
+                             ("on0", 0.0, {3: -1, 11: -1, 12: -1}), ("on1", 0.0, {3: -1, 11: 1, 13: -1}),
+                             ("on2", 0.0, {3: -1, 12: 1, 13: 1}), ("ong", 0.0, {3: -8}), ("ono", 0.0, {3: 4, 11: 2, 12: 2, 13: 2})):
+        fill(om(n), base, n)
+        for r, w in special.items():
+            fill(om(n, r, 16), float(w), n)
+    cp(T.rb[:], T.rel0[:], "rel0", "rb")
+    for r in (5, 6, 7):
+        cp(T.rb[:, r::16], T.rel1[:, r::16], "rel1", "rb")
+    for r in (8, 9, 10):
+        cp(T.rb[:, r::16], T.rel4[:, r::16], "rel4", "rb")
+    for k in "012g":
+        tt(om("w" + k), T.rb[:], om("om" + k), A.mult, "rb om" + k, "w" + k)
+        tt(om("u" + k), T.rel0[:], om("on" + k), A.mult, "rel0 on" + k, "u" + k)
+    tt(om("wo"), T.rel0[:], om("omo"), A.mult, "rel0 omo", "wo")
+    tt(om("uo"), T.rel0[:], om("ono"), A.mult, "rel0 ono", "uo")
+
+    def sum3(dst, keys, src, vn):
+        for k in range(3):
+            act(om("tm%d" % k), om("%s%d" % (src, k)), "%s%d kct" % (src, k), "tm%d" % k, scale=vec("%s%d" % (vn, k)))
+        tt(om("tm0"), om("tm0"), om("tm1"), A.add, "tm0 tm1", "tm0")
+        tt(dst, om("tm0"), om("tm2"), A.add, "tm0 tm2 " + keys.split("_")[0], keys)
+
+    for c, w in (("cm", "w"), ("cmw", "u")):
+        for k in range(3):
+            act(T[c][:, k::4], om("%s%d" % (w, k)), "%s%d kct" % (w, k), "%s_%d" % (c, k), scale=vec("g%d" % k))
+        sum3(T[c][:, 3::4], c + "_3", w, "x")
+        quant("q" + c, T[c][:], "%s_0 %s_1 %s_2 %s_3" % (c, c, c, c))
+    sum3(T.cs[:, 1::4], "cs_", "w", "s")
+    quant("qcs", T.cs[:], "cs cs_")
+    for n, bit in (("1", "b0"), ("2", "b2")):
+        ts(col("le" + n), vec("i0"), 4.0, A.mult, "kct c_" + bit, "c_le" + n, col(bit), A.mult)
+        ts(col("lx" + n), vec("i0"), 4.0, A.mult, "kct", "c_lx" + n)
+        tt(col("lt" + n), col("lx" + n), col("le" + n), A.subtract, "c_lx%s c_le%s" % (n, n), "c_lt" + n)
+        k = 2 * (int(n) - 1)
+        act(T.ci1[:, k::4], om("w" + n), "w%s c_lt%s" % (n, n), "ci1_%d" % k, scale=col("lt" + n))
+        act(T.ci1[:, k + 1::4], om("w" + n), "w%s c_le%s" % (n, n), "ci1_%d" % (k + 1), scale=col("le" + n))
+    act(T.ci2[:, 0::4], om("w0"), "w0 c_lx1 ci2", "ci2_", scale=col("lx1"))
+    quant("qci1", T.ci1[:], "ci1_0 ci1_1 ci1_2 ci1_3")
+    quant("qci2", T.ci2[:], "ci2 ci2_")
+    for c, w in (("cb", "w"), ("cbw", "u")):
+        act(T[c][:, 0::4], om(w + "g"), "%s %sg kct" % (c, w), c + "_0", scale=vec("i0"))
+        act(T[c][:, 1::4], om(w + "o"), "%s %so kct" % (c, w), c + "_1", scale=vec("i0"))
+        quant("q" + c, T[c][:], "%s %s_0 %s_1" % (c, c, c))
+    for k in range(3):
+        r = 11 + k
+        ts(T.cpw[:, 4 * r + 1 + k::64], T.rel0[:, r::16], vec("i0"), A.mult, "rel0 kct", "cpw", -2.0, A.mult)
+    quant("qcpw", T.cpw[:], "cpw")
+    act(T.ck[:, 0::4], T.rel0[:], "rel0 kct ck", "ck_", scale=vec("kv"))
+    quant("qck", T.ck[:], "ck ck_")
+    ts(T.ckg[:, 0::4], T.rel0[:], vec("i0"), A.mult, "rel0 kct", "ckg", 8.0, A.mult)
+    quant("qckg", T.ckg[:], "ckg")
+    ts(T.cn2[:, 0::4], T.rel0[:], vec("bb"), A.mult, "rel0 kct", "cn2")
+    ts(T.cn2[:, 1::4], T.rel0[:], vec("bb"), A.mult, "rel0 kct", "cn2", 8.0, A.mult)
+    quant("qcn2", T.cn2[:], "cn2")
+    quant("qv", T.vt[:], "vt")
+    for t in range(R):
+        quant("aq%d" % t, T.zero[:], "zero", k="aqz%d" % t, a=64, b=192)
+    ts(T.nat[:], T.inat[:], col("b3"), A.add, "inat c_b3", "nat")
+    for k in range(3):
+        tt(T.lwd[:, 20 * k:20 * k + 20], T.lki[:, 20 * k:20 * k + 20], T.nat[:], A.subtract, "lki nat", "lwd%d" % k)
+        if k:
+            ts(T.lwd[:, 20 * k:20 * k + 20], T.lwd[:, 20 * k:20 * k + 20], col("m%d" % k), A.add, "lwd%d c_m%d" % (k, k), "lwd%d" % k)
+        fill(T.kcst[:, 20 * k:20 * k + 20], (0, 1, 6)[k], "kcst")
+    ts(T.nat[:], T.inat[:], col("oa"), A.add, "inat c_oa", "nat")
+    LWD = "lwd0 lwd1 lwd2"
+
+    def table(out, ok, src, reads, n=C, add=None):
+        tt(T.mk[:, 0:n], src, T.mask[:, 0:n], A.mult, reads + " mask", "mk")
+        op("v", "mk sc0", "sc", lambda e: e.tensor_tensor_scan(T.sc[:, 0:n], T.sc0[:, 0:n], T.mk[:, 0:n], 0.0, A.mult, A.add))
+        if add is None:
+            cp(out, T.sc[:, 15:n:16], "sc", ok)
+        else:
+            ts(out, T.sc[:, 15:n:16], add[0], A.add, "sc " + add[1], ok)
+
+    def spread4(dst, src, w, qs):
+        m, i = [], 0
+        for h in range(8):
+            a = (h & 1) + 2 * (h >> 2)
+            for x in (0, 1, 4, 5):
+                d = h ^ x
+                m.append((qs[i % len(qs)], dst[16 * d:16 * d + 16, w * a:w * a + w], src[16 * h:16 * h + 16, 0:w]))
+                i += 1
+        return m
+
+    def lks(k, a=0, b=20):
+        return T.lk16[:, 20 * k + a:20 * k + b]
+
+    def nsw(k):
+        return T.ns[:, 320 * k:320 * k + 320]
+
+    FO, F4 = ("foa", "foa", "fob", "fob"), ("f4a", "f4a", "f4b", "f4b")
+
+    for t in range(R):
+        now, old = "%d" % (t % 2), "%d" % ((t + 1) % 2)
+        quant("qx", T.xt[:], "xt")
+        for bank, la in ((5, 512), (6, 512), (4, 384), (1, 0), (2, 128), (3, 256)):
+            mm(bank, "ua", "qx", True, True, la=la, lk="uac uas")
+        op("v", "ps5", "tc", lambda e: e.transpose(T.tc[:], ps(5)))
+        op("v", "ps4", "tb", lambda e: e.transpose(T.tb[:], ps(4)))
+        tt(T.eqo[:], ps(5), T.tc[:], A.is_equal, "ps5 tc", "eqo")
+        tt(T.eqe[:], ps(4), T.tb[:], A.is_equal, "ps4 tb", "eqe")
+        for s, n in ((0, "eqe"), (1, "eqo")):
+            for a in range(4):
+                h = slice(32 * a, 32 * a + 32)
+                asel(T.rt5[h, s::4], T[n][h, :], [[0, 10], [1, 32]], A.is_gt, 0, -1, n + " rt5", "rt5_%d%d" % (s, a))
+        if t == 0:
+            iota(T.iot[:], [[1, 2560]], 0, 0, "iot", True)
+            iota(T.num[:], [[1280, 2], [320, 2], [1, 640]], 0, 0, "num", True)
+            for k in range(3):
+                act(nsw(k), ps(1 + k), "ps%d" % (1 + k), "ns%d" % k)
+            act(T.srt[:], ps(1), "ps1", "srt")
+        for b in range(10):
+            e = 32 * b + 32
+            sg = "sg" + "ab"[b % 2]
+            act(T[sg][:], ps(6), "ps6 tc", sg, f=F.Sign, scale=-1.0, bias=T.tc[:, 32 * b:32 * b + 1])
+            n, s = "rt%d" % (b // 2), 2 + b % 2
+            act(T[n][:, s:4 * e:4], T[sg][:, 0:e], sg, "%s_%d" % (n, s), f=F.Sign, scale=-1.0, bias=-0.5)
+            if e < C:
+                act(T[n][:, 4 * e + s::4], T[sg][:, e:C], sg, "%s_%dx" % (n, s), f=F.Sign, scale=-1.0, bias=0.5)
+            else:
+                lastw["%s_%dx" % (n, s)] = []
+        rk = 0
+
+        def count(q, last=False):
+            n = "rt%d" % q
+            keys = " ".join("%s_%d" % (n, s) for s in range(4)) + " " + " ".join("%s_%dx" % (n, s) for s in range(4))
+            if q == 5:
+                keys = "rt5 " + " ".join("rt5_%d%d" % (s, a) for s in range(2) for a in range(4))
+            d = ("ra_", "rb_")[q % 2]
+            quant(d, T[n][:], keys)
+            mm(7, "qcr5" if q == 5 else "qcr", d, q == 0, q == 5)
+
+        for b in range(10):
+            e = 32 * b + 32
+            n, s = "rt%d" % (b // 2), b % 2
+            p = T.tb[:, 32 * b:32 * b + 1]
+            ts(T[n][:, s:4 * e:4], ps(4, 0, e), p, A.is_gt, "ps4 tb", "%s_%d" % (n, s))
+            if e < C:
+                ts(T[n][:, 4 * e + s::4], ps(4, e, C), p, A.is_ge, "ps4 tb", "%s_%dx" % (n, s))
+            else:
+                lastw["%s_%dx" % (n, s)] = []
+            if b in (5, 7, 9):
+                count(rk)
+                rk += 1
+        if t == 0:
+            own = T.srt[:]
+            for k in (1, 2):
+                for s, f in ((0, A.is_lt), (1, A.is_le)):
+                    i = 2 * (k - 1) + s
+                    tt(T.flg[:, i::4], nsw(k).indirect(lks(k)), own, f, "srt ns%d lk16" % k, "flg")
+            quant("sq", T.flg[:], "flg")
+            mm(0, "qci1", "sq", True, False)
+            cp(T.lrow[:], T.ioj[:].indirect(lks(0)), "ioj lk16", "lrow")
+            tt(T.lrow[:], T.lrow[:], T.ioj[:], A.is_lt, "lrow ioj", "lrow")
+            tt(T.g1[:], nsw(0).indirect(lks(0)), own, A.is_le, "srt ns0 lk16", "g1")
+            tt(T.g2[:], nsw(0).indirect(lks(0)), own, A.is_lt, "srt ns0 lk16", "g2")
+            tt(T.g1[:], T.g1[:], T.lrow[:], A.min, "g1 lrow", "g1")
+            fill(T.flg[:], 0.0, "flg")
+            tt(T.flg[:, 0::4], T.g1[:], T.g2[:], A.max, "g1 g2", "flg")
+            quant("sq", T.flg[:], "flg")
+            mm(0, "qci2", "sq", False, False)
+            tt(T.gp[:, 1::4], T.tb[:], T.tb[:], A.is_equal, "tb gp", "gp_1")
+            fill(T.flg[:, 0::4], 0.0, "flg")
+        while rk < 6:
+            count(rk)
+            rk += 1
+        ts(T.gp[:, 0::4], ps(7), col("t63"), A.is_lt, "ps7 c_t63 gp", "gp_0")
+        quant("gq" + now, T.gp[:], "gp gp_0 gp_1")
+        if t:
+            mm(0, "qcs", "kq", True, False)
+        mm(0, "qcb", "gq" + now, False, True)
+        for b in range(4):
+            mm((1, 2, 3, 4)[b] if t == 0 else (4, 5, 6, 4)[b], "eb", "qx", True, True, la=128 * b)
+            bank = (1, 2, 3, 4)[b] if t == 0 else (4, 5, 6, 4)[b]
+            act(T[FO[b]][:, 320 * (b % 2):320 * (b % 2) + 320], ps(bank), "ps%d" % bank, "%s_%d" % (FO[b], b % 2))
+            if b % 2:
+                n = FO[b]
+                dma(spread4(T[F4[b]], T[n], 640, "y"), "fd%d" % t, "%s_0 %s_1" % (n, n), F4[b])
+        ex = {i: [] for i in range(6)}
+
+        def later(i):
+            def put(fn):
+                ex[i].append(fn)
+            return put
+
+        @later(0)
+        def _():
+            table(T.rw[:], "rw", ps(7), "ps7", add=(col("off"), "c_off"))
+
+        @later(1)
+        def _():
+            op("v", "rw ioj", "srt", lambda e: e.tensor_copy(T.srt[:].indirect(T.rw[:]), T.ioj[:]))
+            table(T.lg[:], "lg", T.srt[:, 0:64], "srt", n=64)
+            for b in range(4):
+                n = FO[b]
+                act(T.et[:, b:256:4], T[n][:, 320 * (b % 2):320 * (b % 2) + 320].indirect(T.lg[:]), "lg et %s_%d" % (n, b % 2), "et_%d" % b, scale=2.0)
+            if t:
+                for k in range(3):
+                    act(nsw(k), ps(1 + k), "ps%d" % (1 + k), "ns%d" % k)
+
+        @later(2)
+        def _():
+            quant("qe%d" % t, T.et[:], "et et_0 et_1 et_2 et_3")
+            settle("g", lastw["qe%d" % t])
+            rid, pid, _ = topo.addr(nxt)
+            m = topo.mask(core, nxt)
+            ne = len(topo.engines(core, nxt))
+            for d, s, bc in (("aq%dc" % t, "qec", True), ("aq%ds" % t, "qes", False)):
+                o, i = T[d][:, 0:64], T[s][:, 128 * t:128 * t + 64]
+                if bc:
+                    o, i = o.bitcast(dt.uint8), i.bitcast(dt.uint8)
+                g.remote_dma(o, i, T.sem["arr%d" % t], T.sem["snt%d" % t], pid, rid, m)
+            tot["arr%d" % t] = 2 * ne
+            tot["snt%d" % t] = 2 * ne
+            lastw["aq%d" % t] = [("arr%d" % t, 2 * ne, {}, "dma")]
+            ts(T.dsrc[:, 320:640], ps(7), col("s1"), A.add, "ps7 c_s1 c_s2", "dsrc_1", col("s2"), A.min)
+
+        @later(3)
+        def _():
+            cp(T.g2[:], nsw(2).indirect(lks(2)), "ns2 lk16", "g2")
+            tt(T.pp[:, 3::4], nsw(1).indirect(lks(1)), T.g2[:], A.is_le, "ns1 lk16 g2", "pp")
+
+        @later(4)
+        def _():
+            tt(T.pp[:, 2::4], nsw(0).indirect(lks(0)), T.g2[:], A.is_le, "ns0 lk16 g2", "pp")
+            cp(T.g1[:], nsw(1).indirect(lks(1)), "ns1 lk16", "g1")
+
+        @later(5)
+        def _():
+            tt(T.pp[:, 1::4], nsw(0).indirect(lks(0)), T.g1[:], A.is_le, "ns0 lk16 g1", "pp")
+            quant("pq" + now, T.pp[:], "pp")
+            for b in range(4):
+                mm(1 + b, "qw", "aq%d" % t, True, True, la=128 * b, n=128, rk="aq%d aqz%d" % (t, t))
+            for b in range(4):
+                act(T.ho[:, 80 * b:80 * b + 64], ps(1 + b, 0, 64), "ho ps%d" % (1 + b), "ho_%d" % b, scale=0.015625)
+            dma(spread4(T.h4, T.ho, 320, "y"), "hd%d" % t, "ho ho_0 ho_1 ho_2 ho_3", "h4")
+
+        for i in range(SWEEPS):
+            ts(T.pub[:], ps(0), vec("lo"), A.max, "ps0 kct", "pub", vec("hi"), A.min)
+            mm(0, "qcb", "gq" + now, True, False)
+            act(T.st[:, 0::4], T.pub[:].indirect(lks(0)), "st pub lk16", "st_0")
+            cp(T.st[:, 1::4], T.pub[:].indirect(lks(1)), "st pub lk16", "st_1")
+            act(T.st[:, 3::4], T.pub[:], "st pub", "st_3")
+            cp(T.st[:, 2:64 * SPLIT:4], T.pub[:].indirect(lks(2, 0, SPLIT)), "st pub lk16", "st_2")
+            act(T.st[:, 64 * SPLIT + 2::4], T.pub[:].indirect(lks(2, SPLIT, 20)), "st pub lk16", "st_2x")
+            quant("sq", T.st[:], "st st_0 st_1 st_2 st_2x st_3")
+            mm(0, "qcm", "sq", False, True)
+            for fn in ex[i]:
+                fn()
+            if i == SWEEPS - 1:
+                mm(5, "qcbw", "gq" + now, True, False)
+                mm(5, "qcpw", "pq" + now, False, False)
+                mm(5, "qcmw", "sq", False, True)
+        act(T.kt[:, 1::4], ps(0), "ps0 kt", "kt_1")
+        ts(T.kt[:, 0::4], ps(5), 0.0, A.max, "ps5 kt", "kt_0", 1.0, A.min)
+        quant("kq", T.kt[:], "kt kt_0 kt_1")
+        mm(6, "qck", "kq", True, False)
+        mm(6, "qckg", "gq" + now, False, True)
+        table(T.ki[:], "ki", ps(6), "ps6")
+        for k in range(3):
+            op("v", "ki", "kb%d" % k, lambda e: e.tensor_scalar(T.kb[:, 20 * k:20 * k + 20], T.ki[:], (11, 13, 14)[k], None, A.bitwise_and))
+        tt(T.kz[:], T.kb[:], T.kcst[:], A.is_equal, "kb0 kb1 kb2 kcst", "kz")
+        tt(T.kd[:], T.kz[:], T.lwd[:], A.mult, "kz " + LWD, "kd")
+        tt(T.dl[:], T.kd[:, 0:20], T.nat[:], A.add, "kd nat", "dl")
+        tt(T.dl2[:], T.kd[:, 20:40], T.kd[:, 40:60], A.add, "kd", "dl2")
+        tt(T.dl[:], T.dl[:], T.dl2[:], A.add, "dl dl2", "dl")
+        cp(T.dl16[:], T.dl[:], "dl", "dl16")
+        act(T.dsrc[:, 0:320], T.iot[:].indirect(T.dl16[:]), "dl16 iot", "dsrc_0")
+        dma(spread4(T.ds4, T.dsrc, 640, "ys"), "dd%d" % t, "dsrc_0 dsrc_1", "ds4")
+
+        def fwin(b):
+            return T[F4[b]][:, 320 * (b % 2):320 * (b % 2) + 2240]
+
+        for b in range(4):
+            act(T.zd[:, 320 * b:320 * b + 320], fwin(b).indirect(T.dl16[:]), "dl16 " + F4[b], "zd%d" % b)
+        cur = "dl16"
+        for n in ("c1", "c2", "e16"):
+            table(T[n][:], n, T.ds4[:, 0:2240].indirect(T[cur][:]), "ds4 " + cur)
+            cur = n
+        table(T.hl[:], "hl", T.ds4[:, 320:2560].indirect(T.e16[:]), "ds4 e16")
+        if t == R - 1:
+            act(T.lrow[:], T.num[:].indirect(T.e16[:]), "num e16", "lrow")
+            act(T.ndr[:, 0:320], T.lrow[:], "lrow c_cl", "ndr_0", f=F.Identity, bias=col("cl"))
+        for b in range(4):
+            tt(T.zz[:, 320 * b:320 * b + 320], fwin(b).indirect(T.e16[:]), T.zd[:, 320 * b:320 * b + 320], A.add, "e16 zd%d %s" % (b, F4[b]), "zz%d" % b)
+        for b in range(4):
+            tt(T.xt[:, b::4], T.h4[:, 80 * b:80 * b + 1040].indirect(T.hl[:]), T.zz[:, 320 * b:320 * b + 320], A.add, "hl h4 zz%d" % b, "xt")
+
+    quant("qx", T.xt[:], "xt")
+    mm(1, "qv", "qx", True, True)
+    dma([("y", T.oc[:], T.qxc[:].bitcast(dt.uint8))] + [("y", T.osc[4 * k:4 * k + 4, :], T.qxs[32 * k:32 * k + 4, :]) for k in range(4)], "oco", "qx", "oc_")
+    act(T.ysb[:], ps(1), "ps1", "ysb")
+    dma([("s", T.y[:], T.ysb[:])], "yo", "ysb", "y_")
+    ts(T.flg[:, 0::4], ps(0), 3.5, A.is_ge, "ps0", "flg")
+    ts(T.flg[:, 1::4], ps(0), 1.0, A.is_equal, "ps0", "flg")
+    quant("kq", T.flg[:], "flg")
+    mm(7, "qcn2", "kq", True, True)
+    cp(T.ndr[:, 320:640], ps(7), "ps7", "ndr_1")
+    dma([("y", T.nd[:, :], T.ndr[0:128:16, :])], "ndo", "ndr_0 ndr_1", "nd_")
+    for sem in sorted(tot):
+        if know["g"].get(sem, 0) < tot[sem]:
+            g.wait_ge(T.sem[sem], tot[sem])

@@ -22,11 +22,14 @@ for _n, _w in (("xt", 1280), ("ut", 512), ("vt", 512), ("sga", 320), ("sgb", 320
                ("f4a", 2560), ("f4b", 2560), ("ho", 320), ("h4", 1280), ("zd", 1280), ("zz", 1280), ("ident", 128),
                ("ones", 128), ("ra", 128), ("rb", 128), ("pe", 128), ("po", 128), ("rel0", 128), ("rel1", 128), ("rel4", 128),
                ("om", 128 * 23), ("ce", 2048), ("flg", 1280)):
+    if _n not in ("sga", "sgb", "foa", "fob", "f4a", "f4b"):
+        _s(_n, _w, BF)
+for _n, _w in (("sg", 640), ("fo", 1280), ("f4", 5120), ("zero", 1280), ("j31", 320), ("tri", 320), ("zt", 960), ("om", 1792)):
     _s(_n, _w, BF)
 for _i in range(6):
     _s("rt%d" % _i, 1280, BF)
-CONSTS = ["cm", "cmw", "ci1", "ci2", "cb", "cbw", "cpw", "cs", "ck", "ckg", "cn2", "cr", "cr5"]
-OM = {_n: 128 * _i for _i, _n in enumerate([_x + _y for _x in ("om", "on", "w", "u") for _y in "012go"] + ["tm0", "tm1", "tm2"])}
+CONSTS = ["cm", "cmw", "ci1", "ci2", "cb", "cbw", "cpw", "cs", "ck", "ckg", "cn2", "cr", "cr5", "cz"]
+OM = {_n: 128 * _i for _i, _n in enumerate([_x + _y for _x in "wu" for _y in "012go"] + ["tm0", "tm1", "tm2", "re"])}
 LOC = {"eb": ("qk", 0, 512)}
 for _i, _n in enumerate(CONSTS):
     _s(_n, 512, BF)
@@ -34,18 +37,20 @@ for _i, _n in enumerate(CONSTS):
 _q("qk", 512 + 128 * len(CONSTS))
 for _i, _n in enumerate(("gq0", "gq1", "pq0", "pq1", "ra_", "rb_", "sq", "kq")):
     LOC[_n] = ("qf", 320 * _i, 320)
-_q("qf", 320 * 8)
+LOC["zq"] = ("qf", 2560, 240)
+_q("qf", 2800)
 for _i in range(R):
     LOC["qe%d" % _i] = ("qe", 128 * _i, 128)
 _q("qe", 128 * R)
-for _n, _w in (("ns", 960), ("tb", 320), ("tc", 320), ("mk", 320), ("sc", 320), ("srt", 320), ("dsrc", 640), ("ds4", 2560),
+for _n, _w in (("ns", 960), ("tb", 320), ("tc", 320), ("mk", 320), ("sc", 320), ("srt", 320), ("ds4", 2560),
                ("iot", 2560), ("num", 2560), ("mask", 320), ("sc0", 320), ("ioj", 320), ("lwd", 60), ("kz", 60), ("kd", 60),
-               ("dl", 20), ("dl2", 20), ("nat", 20), ("cols", 32), ("kc0", 448), ("kct", 448), ("g1", 320), ("g2", 320),
+               ("dl", 20), ("nat", 20), ("io47", 128), ("lwd4", 240), ("nat4", 80), ("kd4", 240), ("sl", 320), ("cols", 32), ("kc0", 448), ("kct", 448), ("g1", 320), ("g2", 320),
                ("ndr", 640), ("ysb", 320), ("lrow", 320)):
     _s(_n, _w, F32)
-for _n, _w in (("lki", 60), ("ki", 20), ("kb", 60), ("kcst", 60), ("ip", 1), ("ib", 8), ("inat", 20), ("imask", 320), ("iu", 40)):
+for _n, _w in (("lki", 60), ("lk4", 240), ("ki4", 80), ("kb4", 240), ("kc4", 240), ("kcst", 60), ("ip", 1), ("ib", 8), ("inat", 20), ("imask", 320), ("iu", 40)):
     _s(_n, _w, I32)
-for _n, _w in (("lk16", 60), ("rw", 20), ("lg", 4), ("dl16", 20), ("c1", 20), ("c2", 20), ("e16", 20), ("hl", 20), ("ul", 40)):
+OFS = {"dl16": (0, 20), "c1": (20, 20), "c2": (40, 20), "e16": (60, 20), "hl": (80, 20), "rw": (100, 20), "lg": (120, 4), "dl4": (124, 80)}
+for _n, _w in (("lk16", 60), ("of", 204), ("ul", 40)):
     _s(_n, _w, U16)
 for _n, _w in (("qu", 128), ("ua", 640), ("qv", 128), ("qw", 512), ("qx", 320)):
     _q(_n, _w)
@@ -54,7 +59,7 @@ for _i in range(R):
 for _i in range(8):
     SCRATCH["ps%d" % _i] = ("psum", [128, 512], F32)
 
-SEMAPHORES = ["sv", "ss", "st_", "sg_", "ldx", "ldu", "ldv", "ldw", "ldl", "ndo", "yo", "oco"]
+SEMAPHORES = ["sv", "ss", "st_", "sg_", "zf1", "zf2", "zf3", "ldl4", "ldx", "ldu", "ldv", "ldw", "ldl", "ndo", "yo", "oco"]
 for _i in range(R):
     SEMAPHORES += ["fd%d" % _i, "dd%d" % _i, "hd%d" % _i, "arr%d" % _i, "snt%d" % _i]
 
@@ -68,6 +73,14 @@ def rank_program(g, core, T, topo):
     CS = {"v": "sv", "s": "ss", "t": "st_", "g": "sg_"}
     tot, know, lastw, readers = {}, {q: {} for q in ENG}, {}, {}
     dmasem = set()
+    hold, pending = [False], []
+
+    def flush():
+        hold[0] = False
+        for x in pending:
+            op(*x)
+        pending.clear()
+
 
     def settle(q, toks):
         want = {}
@@ -106,6 +119,9 @@ def rank_program(g, core, T, topo):
             readers[w] = []
 
     def op(q, reads, writes, fn):
+        if hold[0] and q != "g":
+            pending.append((q, reads, writes, fn))
+            return
         reads, writes = reads.split(), writes.split()
         sem = CS[q]
         pool = [(sem, tot[sem], {}, q)] if q == "g" and sem in tot else []
@@ -173,11 +189,35 @@ def rank_program(g, core, T, topo):
     def om(n, a=0, st=1):
         return T.om[:, OM[n] + a:OM[n] + 128:st]
 
-    dma([("y", T.xt[:], T.x[:])], "ldx", "", "xt")
+    def u(n, a=0, b=None):
+        o, w = OFS[n]
+        return T.of[:, o + a:o + (w if b is None else b)]
+
+    def lks(k, a=0, b=20):
+        return T.lk16[:, 20 * k + a:20 * k + b]
+
     dma([("s", T.ut[:], T.u[:])], "ldu", "", "ut")
+    dma([("y", T.xt[:], T.x[:])], "ldx", "", "xt")
     dma([("s", T.lki[:], T.lk[:])], "ldl", "", "lki")
+    fill(T.ones[:], 1.0, "ones")
+    fill(T.zero[:], 0.0, "zero")
+    cp(T.lk16[:], T.lki[:], "lki", "lk16")
+
+    def zeros(sem, names):
+        dma([("y", T[n][:, a:min(a + 1280, w)], T.zero[:, 0:min(1280, w - a)]) for n in names.split() for w in [SCRATCH[n][1][1]]
+             for a in range(0, w, 1280)], sem, "zero", names)
+
+    zeros("zf1", "om cr5 rt5 ce")
+    zeros("zf2", "ci2 gp kt cb")
+    zeros("zf3", "cs cbw cpw ck ckg cn2 cz pp et ho zt")
     dma([("y", T.qwc[:].bitcast(dt.uint8), T.wc[:]), ("y", T.qws[:], T.ws[:])], "ldw", "", "qw")
-    dma([("s", T.vt[:], T.v[:])], "ldv", "", "vt")
+    L4 = []
+    for h in range(8):
+        for d in (h, h ^ 1, h ^ 4, h ^ 5):
+            a = (h & 1) + 2 * (h >> 2)
+            L4.append(("y", T.lk4[16 * d:16 * d + 16, 60 * a:60 * a + 60], T.lki[16 * h:16 * h + 16, :]))
+    dma(L4, "ldl4", "lki", "lk4")
+    dma([("y", T.vt[:], T.v[:])], "ldv", "", "vt")
 
     def iota(o, pat, base, ch, w, fl=False):
         if fl:
@@ -188,7 +228,6 @@ def rank_program(g, core, T, topo):
     def asel(o, i, pat, cmp, base, ch, r, w):
         op("g", r, w, lambda e: e.affine_select(o, i, pat, cmp, 0.0, base, ch))
 
-    fill(T.ones[:], 1.0, "ones")
     for k, pat in enumerate(([[16, 8]], [[32, 4], [-16, 2]], [[-64, 2], [16, 4]], [[32, 4], [0, 2]], [[32, 4], [0, 2]])):
         iota(T.iu[:, 8 * k:8 * k + 8], pat, (0, 16, 64, 0, 16)[k], 0, "iu%d" % k)
     iota(T.ip[:], [[0, 1]], 0, 1, "ip")
@@ -208,6 +247,10 @@ def rank_program(g, core, T, topo):
     for i, (sh, an) in enumerate(((4, 1), (5, 1), (6, 1), (0, 15))):
         op("v", "ip", "ib%d" % i, lambda e: e.tensor_scalar(T.ib[:, i:i + 1], T.ip[:], sh, an, A.logical_shift_right, A.bitwise_and))
         cp(col("b%d" % i), T.ib[:, i:i + 1], "ib%d" % i, "c_b%d" % i)
+    ts(col("p31"), col("b0"), 16.0, A.mult, "c_b0 c_b3", "c_p31", col("b3"), A.add)
+    iota(T.j31[:], [[0, 10], [1, 32]], 0, 0, "j31", True)
+    ts(T.tri[:], T.j31[:], col("p31"), A.is_gt, "j31 c_p31", "tri")
+    hold[0] = True
     ts(col("a640"), col("b2"), 2.0, A.mult, "c_b2 c_b0", "c_a2", col("b0"), A.add)
     ts(col("off"), col("b0"), 160.0, A.mult, "c_b0", "c_off")
     ts(col("t63"), col("b0"), -160.0, A.mult, "c_b0", "c_t63", 63.5, A.add)
@@ -217,6 +260,9 @@ def rank_program(g, core, T, topo):
     ts(col("m2"), col("b2"), -2560.0, A.mult, "c_b2", "c_m2", 1280.0, A.add)
     ts(col("cl"), col("b1"), 640.0, A.mult, "c_b1", "c_cl")
     ts(col("oa"), col("a640"), 640.0, A.mult, "c_a2 c_b3", "c_oa", col("b3"), A.add)
+    for a in range(4):
+        ts(col("n%d" % a), col("a640"), float(a), A.not_equal, "c_a2", "c_n%d" % a, 100.0, A.mult)
+    ts(col("p47"), col("b1"), 32.0, A.mult, "c_b1 c_b3", "c_p47", col("b3"), A.add)
     fill(T.kc0[:], 0.0, "kc0")
     VEC = {"g0": {0: -3, 3: -3, 4: 3}, "g1": {5: -3, 6: -3, 7: 3}, "g2": {8: -3, 9: -3, 10: 3}, "x0": {0: 5, 3: 3, 4: -4, 11: 1},
            "x1": {1: 5, 3: 3, 4: -4, 12: 1}, "x2": {2: 5, 3: 3, 4: -4, 13: 1}, "i0": {0: 1}, "kv": {11: 1, 12: 2, 13: 4, 3: 8},
@@ -242,45 +288,39 @@ def rank_program(g, core, T, topo):
     asel(T.pe[:], T.rb[:], [[0, 4], [1, 2], [0, 16]], A.is_equal, 0, 0, "rb", "pe")
     asel(T.po[:], T.rb[:], [[0, 4], [1, 2], [0, 16]], A.not_equal, 0, 0, "rb", "po")
     asel(T.ident[:], T.ones[:], [[-1, 128]], A.is_equal, 0, 1, "ones", "ident")
-
-    for n in ("cr5", "ce", "ci2", "ck", "ckg", "cn2", "cs", "cb", "cbw", "cpw"):
-        fill(T[n][:], 0.0, n)
+    for a in (0, 64):
+        iota(T.io47[:, a:a + 64], [[32, 2], [0, 2], [1, 16]], 0, 0, "io47%d" % a, True)
+    ts(T.cz[:, 0::4], T.io47[:], col("p47"), A.is_equal, "io470 io4764 c_p47 cz", "cz_")
+    quant("qcz", T.cz[:], "cz cz_")
+    hold[0] = False
     act(T.cr[:, 0::4], T.pe[:], "pe", "cr_0")
     act(T.cr[:, 1::4], T.pe[:], "pe", "cr_1")
     act(T.cr[:, 2::4], T.po[:], "po", "cr_2", scale=0.5)
     act(T.cr[:, 3::4], T.po[:], "po", "cr_3", scale=0.5)
     act(T.cr5[:, 0::4], T.pe[:], "pe", "cr5")
     act(T.cr5[:, 1::4], T.po[:], "po cr5", "cr5_")
-    quant("qcr", T.cr[:], "cr_0 cr_1 cr_2 cr_3")
-    quant("qcr5", T.cr5[:], "cr5 cr5_")
+    hold[0] = True
     op("v", "imask", "imask", lambda e: e.tensor_scalar(T.imask[:], T.imask[:], 15, None, A.bitwise_and))
     ts(T.mask[:], T.imask[:], 0.0, A.is_equal, "imask", "mask")
     fill(T.sc0[:], 1.0, "sc0")
     fill(T.sc0[:, 0:C:16], 0.0, "sc0")
-    cp(T.lk16[:], T.lki[:], "lki", "lk16")
-    for z in ("gp", "pp", "st", "kt", "flg", "rt5", "et", "zero", "ho"):
-        fill(T[z][:], 0.0, z)
     for b in range(4):
         act(T.ce[:, 512 * b + b:512 * b + 512:4], T.ident[:], "ident ce", "ce_%d" % b, scale=0.5)
     quant("eb", T.ce[:], "ce ce_0 ce_1 ce_2 ce_3")
-    Z = {11: 0, 12: 0, 13: 0, 14: 0, 15: 0}
-    for n, base, special in (("om0", -1.0, {**Z, 0: -4, 11: 1}), ("om1", -1.0, {**Z, 1: -4, 5: -4, 12: 1}),
-                             ("om2", -1.0, {**Z, 2: -4, 8: -4, 13: 1}), ("omg", -8.0, Z), ("omo", 4.0, {**Z, 4: 3, 7: 3, 10: 3}),
-                             ("on0", 0.0, {3: -1, 11: -1, 12: -1}), ("on1", 0.0, {3: -1, 11: 1, 13: -1}),
-                             ("on2", 0.0, {3: -1, 12: 1, 13: 1}), ("ong", 0.0, {3: -8}), ("ono", 0.0, {3: 4, 11: 2, 12: 2, 13: 2})):
-        fill(om(n), base, n)
+    def rel(r):
+        return "rel0" if r < 5 or r > 10 else "rel1" if r < 8 else "rel4"
+
+    for r in range(11):
+        act(om("re", r, 16), T[rel(r)][:, r::16], "om " + rel(r), "re%d" % r)
+    RE = " ".join("re%d" % r for r in range(11))
+    for n, base, special in (("w0", -1.0, {0: -4, 11: 1}), ("w1", -1.0, {1: -4, 5: -4, 12: 1}), ("w2", -1.0, {2: -4, 8: -4, 13: 1}),
+                             ("wg", -8.0, {}), ("wo", 4.0, {4: 3, 7: 3, 10: 3}), ("u0", 0.0, {3: -1, 11: -1, 12: -1}),
+                             ("u1", 0.0, {3: -1, 11: 1, 13: -1}), ("u2", 0.0, {3: -1, 12: 1, 13: 1}), ("ug", 0.0, {3: -8}),
+                             ("uo", 0.0, {3: 4, 11: 2, 12: 2, 13: 2})):
+        if base:
+            act(om(n), om("re"), RE + " om", n, scale=base)
         for r, w in special.items():
-            fill(om(n, r, 16), float(w), n)
-    cp(T.rb[:], T.rel0[:], "rel0", "rb")
-    for r in (5, 6, 7):
-        cp(T.rb[:, r::16], T.rel1[:, r::16], "rel1", "rb")
-    for r in (8, 9, 10):
-        cp(T.rb[:, r::16], T.rel4[:, r::16], "rel4", "rb")
-    for k in "012g":
-        tt(om("w" + k), T.rb[:], om("om" + k), A.mult, "rb om" + k, "w" + k)
-        tt(om("u" + k), T.rel0[:], om("on" + k), A.mult, "rel0 on" + k, "u" + k)
-    tt(om("wo"), T.rel0[:], om("omo"), A.mult, "rel0 omo", "wo")
-    tt(om("uo"), T.rel0[:], om("ono"), A.mult, "rel0 ono", "uo")
+            act(om(n, r, 16), T[rel(r)][:, r::16], "om " + rel(r), n, scale=float(w))
 
     def sum3(dst, keys, src, vn):
         for k in range(3):
@@ -322,15 +362,27 @@ def rank_program(g, core, T, topo):
     quant("qcn2", T.cn2[:], "cn2")
     quant("qv", T.vt[:], "vt")
     for t in range(R):
-        quant("aq%d" % t, T.zero[:], "zero", k="aqz%d" % t, a=64, b=192)
-    ts(T.nat[:], T.inat[:], col("b3"), A.add, "inat c_b3", "nat")
-    for k in range(3):
-        tt(T.lwd[:, 20 * k:20 * k + 20], T.lki[:, 20 * k:20 * k + 20], T.nat[:], A.subtract, "lki nat", "lwd%d" % k)
-        if k:
-            ts(T.lwd[:, 20 * k:20 * k + 20], T.lwd[:, 20 * k:20 * k + 20], col("m%d" % k), A.add, "lwd%d c_m%d" % (k, k), "lwd%d" % k)
-        fill(T.kcst[:, 20 * k:20 * k + 20], (0, 1, 6)[k], "kcst")
-    ts(T.nat[:], T.inat[:], col("oa"), A.add, "inat c_oa", "nat")
+        quant("aq%d" % t, T.zero[:, 0:512], "zero", k="aqz%d" % t, a=64, b=192)
+    def routes_tables():
+        ts(T.nat[:], T.inat[:], col("b3"), A.add, "inat c_b3", "nat")
+        for k in range(3):
+            sl = slice(20 * k, 20 * k + 20)
+            tt(T.lwd[:, sl], T.lki[:, sl], T.nat[:], A.subtract, "lki nat", "lwd%d" % k)
+            if k:
+                ts(T.lwd[:, sl], T.lwd[:, sl], col("m%d" % k), A.add, "lwd%d c_m%d" % (k, k), "lwd%d" % k)
+            fill(T.kcst[:, sl], (0, 1, 6)[k], "kcst")
+            for a in range(4):
+                s4 = slice(80 * k + 20 * a, 80 * k + 20 * a + 20)
+                tt(T.lwd4[:, s4], T.lk4[:, 60 * a + 20 * k:60 * a + 20 * k + 20], T.nat[:], A.subtract, "lk4 nat", "lwd4%d%d" % (k, a))
+                if k:
+                    act(T.lwd4[:, s4], T.lwd4[:, s4], "lwd4%d%d" % (k, a), "lwd4%d%d" % (k, a), f=F.Identity, bias=640.0 * ((a ^ k) - a))
+                ts(T.kc4[:, s4], T.kcst[:, sl], col("n%d" % a), A.add, "kcst c_n%d" % a, "kc4")
+        for a in range(4):
+            act(T.nat4[:, 20 * a:20 * a + 20], T.nat[:], "nat", "nat4", f=F.Identity, bias=640.0 * a)
+        ts(T.nat[:], T.inat[:], col("oa"), A.add, "inat c_oa", "nat")
+
     LWD = "lwd0 lwd1 lwd2"
+    LWD4 = " ".join("lwd4%d%d" % (k, a) for k in range(3) for a in range(4))
 
     def table(out, ok, src, reads, n=C, add=None):
         tt(T.mk[:, 0:n], src, T.mask[:, 0:n], A.mult, reads + " mask", "mk")
@@ -340,24 +392,19 @@ def rank_program(g, core, T, topo):
         else:
             ts(out, T.sc[:, 15:n:16], add[0], A.add, "sc " + add[1], ok)
 
-    def spread4(dst, src, w, qs):
-        m, i = [], 0
+    def spread4(dst, src, w, do=0, so=0, pitch=None):
+        m = []
         for h in range(8):
-            a = (h & 1) + 2 * (h >> 2)
-            for x in (0, 1, 4, 5):
-                d = h ^ x
-                m.append((qs[i % len(qs)], dst[16 * d:16 * d + 16, w * a:w * a + w], src[16 * h:16 * h + 16, 0:w]))
-                i += 1
+            a = do + (pitch or w) * ((h & 1) + 2 * (h >> 2))
+            for d in (h, h ^ 1, h ^ 4, h ^ 5):
+                m.append(("y", dst[16 * d:16 * d + 16, a:a + w], src[16 * h:16 * h + 16, so:so + w]))
         return m
-
-    def lks(k, a=0, b=20):
-        return T.lk16[:, 20 * k + a:20 * k + b]
 
     def nsw(k):
         return T.ns[:, 320 * k:320 * k + 320]
 
-    FO, F4 = ("foa", "foa", "fob", "fob"), ("f4a", "f4a", "f4b", "f4b")
 
+    hold[0] = False
     for t in range(R):
         now, old = "%d" % (t % 2), "%d" % ((t + 1) % 2)
         quant("qx", T.xt[:], "xt")
@@ -367,7 +414,7 @@ def rank_program(g, core, T, topo):
         op("v", "ps4", "tb", lambda e: e.transpose(T.tb[:], ps(4)))
         tt(T.eqo[:], ps(5), T.tc[:], A.is_equal, "ps5 tc", "eqo")
         tt(T.eqe[:], ps(4), T.tb[:], A.is_equal, "ps4 tb", "eqe")
-        for s, n in ((0, "eqe"), (1, "eqo")):
+        for s, n in ((1, "eqo"),):
             for a in range(4):
                 h = slice(32 * a, 32 * a + 32)
                 asel(T.rt5[h, s::4], T[n][h, :], [[0, 10], [1, 32]], A.is_gt, 0, -1, n + " rt5", "rt5_%d%d" % (s, a))
@@ -377,14 +424,15 @@ def rank_program(g, core, T, topo):
             for k in range(3):
                 act(nsw(k), ps(1 + k), "ps%d" % (1 + k), "ns%d" % k)
             act(T.srt[:], ps(1), "ps1", "srt")
+            act(T.lrow[:], T.ioj[:].indirect(lks(0)), "ioj lk16", "lrow")
         for b in range(10):
             e = 32 * b + 32
-            sg = "sg" + "ab"[b % 2]
-            act(T[sg][:], ps(6), "ps6 tc", sg, f=F.Sign, scale=-1.0, bias=T.tc[:, 32 * b:32 * b + 1])
+            sg, so = "sg%d" % (b % 2), 320 * (b % 2)
+            act(T.sg[:, so:so + 320], ps(6), "ps6 tc", sg, f=F.Sign, scale=-1.0, bias=T.tc[:, 32 * b:32 * b + 1])
             n, s = "rt%d" % (b // 2), 2 + b % 2
-            act(T[n][:, s:4 * e:4], T[sg][:, 0:e], sg, "%s_%d" % (n, s), f=F.Sign, scale=-1.0, bias=-0.5)
+            act(T[n][:, s:4 * e:4], T.sg[:, so:so + e], sg, "%s_%d" % (n, s), f=F.Sign, scale=-1.0, bias=-0.5)
             if e < C:
-                act(T[n][:, 4 * e + s::4], T[sg][:, e:C], sg, "%s_%dx" % (n, s), f=F.Sign, scale=-1.0, bias=0.5)
+                act(T[n][:, 4 * e + s::4], T.sg[:, so + e:so + C], sg, "%s_%dx" % (n, s), f=F.Sign, scale=-1.0, bias=0.5)
             else:
                 lastw["%s_%dx" % (n, s)] = []
         rk = 0
@@ -393,11 +441,12 @@ def rank_program(g, core, T, topo):
             n = "rt%d" % q
             keys = " ".join("%s_%d" % (n, s) for s in range(4)) + " " + " ".join("%s_%dx" % (n, s) for s in range(4))
             if q == 5:
-                keys = "rt5 " + " ".join("rt5_%d%d" % (s, a) for s in range(2) for a in range(4))
+                keys = "rt5 rt5_0 " + " ".join("rt5_1%d" % a for a in range(4))
             d = ("ra_", "rb_")[q % 2]
             quant(d, T[n][:], keys)
             mm(7, "qcr5" if q == 5 else "qcr", d, q == 0, q == 5)
 
+        tt(T.rt5[:, 0::4], T.eqe[:], T.tri[:], A.mult, "eqe tri rt5", "rt5_0")
         for b in range(10):
             e = 32 * b + 32
             n, s = "rt%d" % (b // 2), b % 2
@@ -408,6 +457,9 @@ def rank_program(g, core, T, topo):
             else:
                 lastw["%s_%dx" % (n, s)] = []
             if b in (5, 7, 9):
+                if t == 0 and b == 5:
+                    quant("qcr", T.cr[:], "cr_0 cr_1 cr_2 cr_3")
+                    quant("qcr5", T.cr5[:], "cr5 cr5_")
                 count(rk)
                 rk += 1
         if t == 0:
@@ -417,33 +469,32 @@ def rank_program(g, core, T, topo):
                     i = 2 * (k - 1) + s
                     tt(T.flg[:, i::4], nsw(k).indirect(lks(k)), own, f, "srt ns%d lk16" % k, "flg")
             quant("sq", T.flg[:], "flg")
-            mm(0, "qci1", "sq", True, False)
-            cp(T.lrow[:], T.ioj[:].indirect(lks(0)), "ioj lk16", "lrow")
             tt(T.lrow[:], T.lrow[:], T.ioj[:], A.is_lt, "lrow ioj", "lrow")
             tt(T.g1[:], nsw(0).indirect(lks(0)), own, A.is_le, "srt ns0 lk16", "g1")
             tt(T.g2[:], nsw(0).indirect(lks(0)), own, A.is_lt, "srt ns0 lk16", "g2")
             tt(T.g1[:], T.g1[:], T.lrow[:], A.min, "g1 lrow", "g1")
-            fill(T.flg[:], 0.0, "flg")
-            tt(T.flg[:, 0::4], T.g1[:], T.g2[:], A.max, "g1 g2", "flg")
-            quant("sq", T.flg[:], "flg")
-            mm(0, "qci2", "sq", False, False)
+            tt(T.kt[:, 0::4], T.g1[:], T.g2[:], A.max, "g1 g2 kt", "kt_0")
+            quant("kq", T.kt[:], "kt kt_0")
             tt(T.gp[:, 1::4], T.tb[:], T.tb[:], A.is_equal, "tb gp", "gp_1")
-            fill(T.flg[:, 0::4], 0.0, "flg")
         while rk < 6:
             count(rk)
             rk += 1
+        if t == 0:
+            flush()
+            mm(0, "qci1", "sq", True, False)
+            mm(0, "qci2", "kq", False, False)
         ts(T.gp[:, 0::4], ps(7), col("t63"), A.is_lt, "ps7 c_t63 gp", "gp_0")
         quant("gq" + now, T.gp[:], "gp gp_0 gp_1")
         if t:
             mm(0, "qcs", "kq", True, False)
         mm(0, "qcb", "gq" + now, False, True)
-        for b in range(4):
-            mm((1, 2, 3, 4)[b] if t == 0 else (4, 5, 6, 4)[b], "eb", "qx", True, True, la=128 * b)
-            bank = (1, 2, 3, 4)[b] if t == 0 else (4, 5, 6, 4)[b]
-            act(T[FO[b]][:, 320 * (b % 2):320 * (b % 2) + 320], ps(bank), "ps%d" % bank, "%s_%d" % (FO[b], b % 2))
+        def unpack(b):
+            bank = (4, 5, 6, 4)[b]
+            mm(bank, "eb", "qx", True, True, la=128 * b)
+            act(T.fo[:, 320 * b:320 * b + 320], ps(bank), "ps%d" % bank, "fo%d" % b)
             if b % 2:
-                n = FO[b]
-                dma(spread4(T[F4[b]], T[n], 640, "y"), "fd%d" % t, "%s_0 %s_1" % (n, n), F4[b])
+                dma(spread4(T.f4, T.fo, 640, do=1280 * (b - 1), so=320 * (b - 1)), "fd%d" % t, "fo%d fo%d" % (b - 1, b), "f4%d" % (b // 2))
+
         ex = {i: [] for i in range(6)}
 
         def later(i):
@@ -453,20 +504,23 @@ def rank_program(g, core, T, topo):
 
         @later(0)
         def _():
-            table(T.rw[:], "rw", ps(7), "ps7", add=(col("off"), "c_off"))
+            table(u("rw"), "rw", ps(7), "ps7", add=(col("off"), "c_off"))
+            unpack(0)
+            unpack(1)
 
         @later(1)
         def _():
-            op("v", "rw ioj", "srt", lambda e: e.tensor_copy(T.srt[:].indirect(T.rw[:]), T.ioj[:]))
-            table(T.lg[:], "lg", T.srt[:, 0:64], "srt", n=64)
-            for b in range(4):
-                n = FO[b]
-                act(T.et[:, b:256:4], T[n][:, 320 * (b % 2):320 * (b % 2) + 320].indirect(T.lg[:]), "lg et %s_%d" % (n, b % 2), "et_%d" % b, scale=2.0)
-            if t:
-                for k in range(3):
-                    act(nsw(k), ps(1 + k), "ps%d" % (1 + k), "ns%d" % k)
+            op("v", "rw ioj", "srt", lambda e: e.tensor_copy(T.srt[:].indirect(u("rw")), T.ioj[:]))
+            unpack(2)
+            unpack(3)
 
         @later(2)
+        def _():
+            table(u("lg"), "lg", T.srt[:, 0:64], "srt", n=64)
+            for b in range(4):
+                act(T.et[:, b:256:4], T.fo[:, 320 * b:320 * b + 320].indirect(u("lg")), "lg et fo%d" % b, "et_%d" % b, scale=2.0)
+
+        @later(3)
         def _():
             quant("qe%d" % t, T.et[:], "et et_0 et_1 et_2 et_3")
             settle("g", lastw["qe%d" % t])
@@ -481,27 +535,37 @@ def rank_program(g, core, T, topo):
             tot["arr%d" % t] = 2 * ne
             tot["snt%d" % t] = 2 * ne
             lastw["aq%d" % t] = [("arr%d" % t, 2 * ne, {}, "dma")]
-            ts(T.dsrc[:, 320:640], ps(7), col("s1"), A.add, "ps7 c_s1 c_s2", "dsrc_1", col("s2"), A.min)
+            if t:
+                act(nsw(2), ps(3), "ps3", "ns2")
+                act(nsw(1), ps(2), "ps2", "ns1")
+            act(T.g2[:], nsw(2).indirect(lks(2)), "ns2 lk16", "g2")
 
-        @later(3)
+        @later(2)
         def _():
-            cp(T.g2[:], nsw(2).indirect(lks(2)), "ns2 lk16", "g2")
-            tt(T.pp[:, 3::4], nsw(1).indirect(lks(1)), T.g2[:], A.is_le, "ns1 lk16 g2", "pp")
+            ts(T.sl[:], ps(7), col("s1"), A.add, "ps7 c_s1 c_s2", "sl", col("s2"), A.min)
+            dma(spread4(T.ds4, T.sl, 320, do=320, pitch=640), "dd%d" % t, "sl", "ds4s")
+            if t == 0:
+                routes_tables()
 
         @later(4)
         def _():
-            tt(T.pp[:, 2::4], nsw(0).indirect(lks(0)), T.g2[:], A.is_le, "ns0 lk16 g2", "pp")
-            cp(T.g1[:], nsw(1).indirect(lks(1)), "ns1 lk16", "g1")
+            tt(T.pp[:, 3::4], nsw(1).indirect(lks(1)), T.g2[:], A.is_le, "ns1 lk16 g2 pp", "pp3")
+            if t:
+                act(nsw(0), ps(1), "ps1", "ns0")
+            act(T.g1[:], nsw(1).indirect(lks(1)), "ns1 lk16", "g1")
 
         @later(5)
         def _():
-            tt(T.pp[:, 1::4], nsw(0).indirect(lks(0)), T.g1[:], A.is_le, "ns0 lk16 g1", "pp")
-            quant("pq" + now, T.pp[:], "pp")
+            tt(T.pp[:, 2::4], nsw(0).indirect(lks(0)), T.g2[:], A.is_le, "ns0 lk16 g2 pp", "pp2")
+            tt(T.pp[:, 1::4], nsw(0).indirect(lks(0)), T.g1[:], A.is_le, "ns0 lk16 g1 pp", "pp1")
+            quant("pq" + now, T.pp[:], "pp pp1 pp2 pp3")
+
+        def layer():
             for b in range(4):
                 mm(1 + b, "qw", "aq%d" % t, True, True, la=128 * b, n=128, rk="aq%d aqz%d" % (t, t))
             for b in range(4):
                 act(T.ho[:, 80 * b:80 * b + 64], ps(1 + b, 0, 64), "ho ps%d" % (1 + b), "ho_%d" % b, scale=0.015625)
-            dma(spread4(T.h4, T.ho, 320, "y"), "hd%d" % t, "ho ho_0 ho_1 ho_2 ho_3", "h4")
+            dma(spread4(T.h4, T.ho, 320), "hd%d" % t, "ho ho_0 ho_1 ho_2 ho_3", "h4")
 
         for i in range(SWEEPS):
             ts(T.pub[:], ps(0), vec("lo"), A.max, "ps0 kct", "pub", vec("hi"), A.min)
@@ -524,35 +588,54 @@ def rank_program(g, core, T, topo):
         quant("kq", T.kt[:], "kt kt_0 kt_1")
         mm(6, "qck", "kq", True, False)
         mm(6, "qckg", "gq" + now, False, True)
-        table(T.ki[:], "ki", ps(6), "ps6")
+        table(T.ki4[:, 0:20], "ki0", ps(6), "ps6")
+        for a in range(1, 4):
+            cp(T.ki4[:, 20 * a:20 * a + 20], T.sc[:, 15:C:16], "sc", "ki%d" % a)
         for k in range(3):
-            op("v", "ki", "kb%d" % k, lambda e: e.tensor_scalar(T.kb[:, 20 * k:20 * k + 20], T.ki[:], (11, 13, 14)[k], None, A.bitwise_and))
-        tt(T.kz[:], T.kb[:], T.kcst[:], A.is_equal, "kb0 kb1 kb2 kcst", "kz")
-        tt(T.kd[:], T.kz[:], T.lwd[:], A.mult, "kz " + LWD, "kd")
+            op("v", "ki0 ki1 ki2 ki3", "kb%d" % k, lambda e: e.tensor_scalar(T.kb4[:, 80 * k:80 * k + 80], T.ki4[:], (11, 13, 14)[k], None, A.bitwise_and))
+        tt(T.zt[:, 0::4], T.kb4[:], T.kc4[:], A.is_equal, "kb0 kb1 kb2 kc4 zt", "zt_")
+        quant("zq", T.zt[:], "zt zt_")
+        mm(5, "qcz", "zq", True, True, n=240)
+        for k in range(3):
+            tt(T.kz[:, 20 * k:20 * k + 20], T.kb4[:, 80 * k:80 * k + 20], T.kcst[:, 20 * k:20 * k + 20], A.is_equal, "kb%d kcst" % k, "kz%d" % k)
+        tt(T.kd4[:], ps(5, 0, 240), T.lwd4[:], A.mult, "ps5 " + LWD4, "kd4")
+        tt(T.kd4[:, 0:80], T.kd4[:, 0:80], T.nat4[:], A.add, "kd4 nat4", "kd4a")
+        tt(T.kd4[:, 80:160], T.kd4[:, 80:160], T.kd4[:, 160:240], A.add, "kd4", "kd4b")
+        tt(T.kd4[:, 0:80], T.kd4[:, 0:80], T.kd4[:, 80:160], A.add, "kd4a kd4b", "kd4c")
+        cp(u("dl4"), T.kd4[:, 0:80], "kd4c", "dl4")
+        lastw["kd4"] = lastw["kd4c"]
+        readers["kd4"] = list(readers.get("kd4c", []))
+        for a in (0, 1):
+            act(T.ds4[:, 640 * a:640 * a + 320], T.iot[:].indirect(u("dl4", 20 * a, 20 * a + 20)), "dl4 iot", "ds4%d" % a)
+        tt(T.kd[:], T.kz[:], T.lwd[:], A.mult, "kz0 kz1 kz2 " + LWD, "kd")
         tt(T.dl[:], T.kd[:, 0:20], T.nat[:], A.add, "kd nat", "dl")
-        tt(T.dl2[:], T.kd[:, 20:40], T.kd[:, 40:60], A.add, "kd", "dl2")
-        tt(T.dl[:], T.dl[:], T.dl2[:], A.add, "dl dl2", "dl")
-        cp(T.dl16[:], T.dl[:], "dl", "dl16")
-        act(T.dsrc[:, 0:320], T.iot[:].indirect(T.dl16[:]), "dl16 iot", "dsrc_0")
-        dma(spread4(T.ds4, T.dsrc, 640, "ys"), "dd%d" % t, "dsrc_0 dsrc_1", "ds4")
+        tt(T.dl[:], T.dl[:], T.kd[:, 20:40], A.add, "dl kd", "dl")
+        tt(T.dl[:], T.dl[:], T.kd[:, 40:60], A.add, "dl kd", "dl")
+        cp(u("dl16"), T.dl[:], "dl", "dl16")
+        for a in (2, 3):
+            cp(T.ds4[:, 640 * a:640 * a + 320], T.iot[:].indirect(u("dl4", 20 * a, 20 * a + 20)), "dl4 iot", "ds4%d" % a)
+        DS = "ds40 ds41 ds42 ds43 ds4s "
 
         def fwin(b):
-            return T[F4[b]][:, 320 * (b % 2):320 * (b % 2) + 2240]
+            o = 2560 * (b // 2) + 320 * (b % 2)
+            return T.f4[:, o:o + 2240]
 
         for b in range(4):
-            act(T.zd[:, 320 * b:320 * b + 320], fwin(b).indirect(T.dl16[:]), "dl16 " + F4[b], "zd%d" % b)
+            act(T.zd[:, 320 * b:320 * b + 320], fwin(b).indirect(u("dl16")), "dl16 f4%d" % (b // 2), "zd%d" % b)
+            if b == 0:
+                layer()
         cur = "dl16"
         for n in ("c1", "c2", "e16"):
-            table(T[n][:], n, T.ds4[:, 0:2240].indirect(T[cur][:]), "ds4 " + cur)
+            table(u(n), n, T.ds4[:, 0:2240].indirect(u(cur)), DS + cur)
             cur = n
-        table(T.hl[:], "hl", T.ds4[:, 320:2560].indirect(T.e16[:]), "ds4 e16")
+        table(u("hl"), "hl", T.ds4[:, 320:2560].indirect(u("e16")), DS + "e16")
         if t == R - 1:
-            act(T.lrow[:], T.num[:].indirect(T.e16[:]), "num e16", "lrow")
+            act(T.lrow[:], T.num[:].indirect(u("e16")), "num e16", "lrow")
             act(T.ndr[:, 0:320], T.lrow[:], "lrow c_cl", "ndr_0", f=F.Identity, bias=col("cl"))
         for b in range(4):
-            tt(T.zz[:, 320 * b:320 * b + 320], fwin(b).indirect(T.e16[:]), T.zd[:, 320 * b:320 * b + 320], A.add, "e16 zd%d %s" % (b, F4[b]), "zz%d" % b)
+            tt(T.zz[:, 320 * b:320 * b + 320], fwin(b).indirect(u("e16")), T.zd[:, 320 * b:320 * b + 320], A.add, "e16 zd%d f4%d" % (b, b // 2), "zz%d" % b)
         for b in range(4):
-            tt(T.xt[:, b::4], T.h4[:, 80 * b:80 * b + 1040].indirect(T.hl[:]), T.zz[:, 320 * b:320 * b + 320], A.add, "hl h4 zz%d" % b, "xt")
+            tt(T.xt[:, b::4], T.h4[:, 80 * b:80 * b + 1040].indirect(u("hl")), T.zz[:, 320 * b:320 * b + 320], A.add, "hl h4 zz%d" % b, "xt")
 
     quant("qx", T.xt[:], "xt")
     mm(1, "qv", "qx", True, True)

@@ -3,7 +3,7 @@ from concourse.mybir import dt, AluOpType as A, ActivationFunctionType as F
 
 C, GW, R, SWEEPS = 320, 64, 3, 6
 BF, F32, I32, U16, X4, U8 = "bfloat16", "float32", "int32", "uint16", "float8_e4m3fn_x4", "uint8"
-SPLIT = 14
+SPLIT = 18
 
 SCRATCH = {}
 
@@ -73,6 +73,7 @@ def rank_program(g, core, T, topo):
     CS = {"v": "sv", "s": "ss", "t": "st_", "g": "sg_"}
     tot, know, lastw, readers = {}, {q: {} for q in ENG}, {}, {}
     dmasem = set()
+    GRP = {"xt": "xt xt0 xt1 xt2 xt3"}
     hold, pending = [False], []
 
     def flush():
@@ -122,6 +123,7 @@ def rank_program(g, core, T, topo):
         if hold[0] and q != "g":
             pending.append((q, reads, writes, fn))
             return
+        reads = " ".join(GRP.get(x, x) for x in reads.split())
         reads, writes = reads.split(), writes.split()
         sem = CS[q]
         pool = [(sem, tot[sem], {}, q)] if q == "g" and sem in tot else []
@@ -201,13 +203,14 @@ def rank_program(g, core, T, topo):
     dma([("s", T.lki[:], T.lk[:])], "ldl", "", "lki")
     fill(T.ones[:], 1.0, "ones")
     fill(T.zero[:], 0.0, "zero")
-    cp(T.lk16[:], T.lki[:], "lki", "lk16")
+    fill(T.cr5[:], 0.0, "cr5")
+    fill(T.rt5[:], 0.0, "rt5")
 
     def zeros(sem, names):
         dma([("y", T[n][:, a:min(a + 1280, w)], T.zero[:, 0:min(1280, w - a)]) for n in names.split() for w in [SCRATCH[n][1][1]]
              for a in range(0, w, 1280)], sem, "zero", names)
 
-    zeros("zf1", "om cr5 rt5 ce")
+    zeros("zf1", "om ce")
     zeros("zf2", "ci2 gp kt cb")
     zeros("zf3", "cs cbw cpw ck ckg cn2 cz pp et ho zt")
     dma([("y", T.qwc[:].bitcast(dt.uint8), T.wc[:]), ("y", T.qws[:], T.ws[:])], "ldw", "", "qw")
@@ -231,9 +234,12 @@ def rank_program(g, core, T, topo):
     for k, pat in enumerate(([[16, 8]], [[32, 4], [-16, 2]], [[-64, 2], [16, 4]], [[32, 4], [0, 2]], [[32, 4], [0, 2]])):
         iota(T.iu[:, 8 * k:8 * k + 8], pat, (0, 16, 64, 0, 16)[k], 0, "iu%d" % k)
     iota(T.ip[:], [[0, 1]], 0, 1, "ip")
-    iota(T.imask[:], [[1, C]], 128, -1, "imask")
-    iota(T.inat[:], [[16, 20]], 0, 0, "inat")
+    asel(T.ra[:], T.ones[:], [[-32, 4], [0, 32]], A.is_ge, 0, 1, "ones", "ra")
+    asel(T.rb[:], T.ra[:], [[32, 4], [0, 32]], A.is_ge, 31, -1, "ra", "rb")
+    asel(T.pe[:], T.rb[:], [[0, 4], [1, 2], [0, 16]], A.is_equal, 0, 0, "rb", "pe")
+    asel(T.po[:], T.rb[:], [[0, 4], [1, 2], [0, 16]], A.not_equal, 0, 0, "rb", "po")
     iota(T.ioj[:], [[1, C]], 0, 0, "ioj", True)
+    iota(T.inat[:], [[16, 20]], 0, 0, "inat")
     cp(T.ul[:], T.iu[:], "iu0 iu1 iu2 iu3 iu4", "ul")
     quant("qu", T.ut[:], "ut")
     op("v", "qu ul", "uac", lambda e: e.tensor_copy(T.uac[:].bitcast(dt.uint32), T.quc[:].bitcast(dt.uint32).indirect(T.ul[:, 0:40])))
@@ -244,16 +250,22 @@ def rank_program(g, core, T, topo):
         cl.setdefault(name, len(cl))
         return T.cols[:, cl[name]:cl[name] + 1]
 
-    for i, (sh, an) in enumerate(((4, 1), (5, 1), (6, 1), (0, 15))):
-        op("v", "ip", "ib%d" % i, lambda e: e.tensor_scalar(T.ib[:, i:i + 1], T.ip[:], sh, an, A.logical_shift_right, A.bitwise_and))
-        cp(col("b%d" % i), T.ib[:, i:i + 1], "ib%d" % i, "c_b%d" % i)
-    ts(col("p31"), col("b0"), 16.0, A.mult, "c_b0 c_b3", "c_p31", col("b3"), A.add)
+    quant("qx", T.xt[:], "xt")
+    cp(T.lk16[:], T.lki[:], "lki", "lk16")
     iota(T.j31[:], [[0, 10], [1, 32]], 0, 0, "j31", True)
-    ts(T.tri[:], T.j31[:], col("p31"), A.is_gt, "j31 c_p31", "tri")
+
+    def bits():
+        for i, (sh, an) in enumerate(((4, 1), (5, 1), (6, 1), (0, 15))):
+            op("v", "ip", "ib%d" % i, lambda e: e.tensor_scalar(T.ib[:, i:i + 1], T.ip[:], sh, an, A.logical_shift_right, A.bitwise_and))
+        for i in range(4):
+            cp(col("b%d" % i), T.ib[:, i:i + 1], "ib%d" % i, "c_b%d" % i)
+        ts(col("p31"), col("b0"), 16.0, A.mult, "c_b0 c_b3", "c_p31", col("b3"), A.add)
+        ts(T.tri[:], T.j31[:], col("p31"), A.is_gt, "j31 c_p31", "tri")
+
     hold[0] = True
     ts(col("a640"), col("b2"), 2.0, A.mult, "c_b2 c_b0", "c_a2", col("b0"), A.add)
-    ts(col("off"), col("b0"), 160.0, A.mult, "c_b0", "c_off")
-    ts(col("t63"), col("b0"), -160.0, A.mult, "c_b0", "c_t63", 63.5, A.add)
+    ts(col("off"), col("b0"), 144.0, A.mult, "c_b0", "c_off")
+    ts(col("t63"), col("b0"), -144.0, A.mult, "c_b0", "c_t63", 63.5, A.add)
     ts(col("s1"), col("a640"), 320.0, A.mult, "c_a2 c_off", "c_s1", col("off"), A.add)
     ts(col("s2"), col("a640"), 320.0, A.mult, "c_a2", "c_s2", 64.0, A.add)
     ts(col("m1"), col("b0"), -1280.0, A.mult, "c_b0", "c_m1", 640.0, A.add)
@@ -267,13 +279,19 @@ def rank_program(g, core, T, topo):
     VEC = {"g0": {0: -3, 3: -3, 4: 3}, "g1": {5: -3, 6: -3, 7: 3}, "g2": {8: -3, 9: -3, 10: 3}, "x0": {0: 5, 3: 3, 4: -4, 11: 1},
            "x1": {1: 5, 3: 3, 4: -4, 12: 1}, "x2": {2: 5, 3: 3, 4: -4, 13: 1}, "i0": {0: 1}, "kv": {11: 1, 12: 2, 13: 4, 3: 8},
            "bb": {11: 1, 12: 2, 13: 4}, "s0": {11: 1}, "s1": {12: 1}, "s2": {13: 1}, "lo": {11: -99, 12: -99, 13: -99}, "hi": {11: 99, 12: 99, 13: 99}}
+    KC = []
+
+    def put(o, v, over, key):
+        op("v", over, key, lambda e: e.memset(o, v))
+
     vi = {n: i for i, n in enumerate(VEC)}
     fill(T.kc0[:, 32 * vi["hi"]:32 * vi["hi"] + 32], 1.0, "kc0")
     for n, d in VEC.items():
         o = 32 * vi[n]
         for r, w in d.items():
-            fill(T.kc0[:, o + r:o + 32:16], float(w), "kc0")
-    op("v", "kc0", "kct", lambda e: e.transpose(T.kct[:], T.kc0[:]))
+            put(T.kc0[:, o + r:o + 32:16], float(w), "kc0", "kc0_%d" % (o + r))
+            KC.append("kc0_%d" % (o + r))
+    op("v", "kc0 " + " ".join(KC), "kct", lambda e: e.transpose(T.kct[:], T.kc0[:]))
 
     def vec(n):
         return T.kct[:, 32 * vi[n]:32 * vi[n] + 1]
@@ -283,22 +301,17 @@ def rank_program(g, core, T, topo):
                               ("rel4", [[64, 2], [-16, 4], [0, 16]], -64, [[-64, 2], [16, 4], [0, 16]], 79)):
         asel(T.ra[:], T.ones[:], p1, A.is_ge, b1, 1, "ones", "ra")
         asel(T[n][:], T.ra[:], p2, A.is_ge, b2, -1, "ra", n)
-    asel(T.ra[:], T.ones[:], [[-32, 4], [0, 32]], A.is_ge, 0, 1, "ones", "ra")
-    asel(T.rb[:], T.ra[:], [[32, 4], [0, 32]], A.is_ge, 31, -1, "ra", "rb")
-    asel(T.pe[:], T.rb[:], [[0, 4], [1, 2], [0, 16]], A.is_equal, 0, 0, "rb", "pe")
-    asel(T.po[:], T.rb[:], [[0, 4], [1, 2], [0, 16]], A.not_equal, 0, 0, "rb", "po")
+    iota(T.imask[:], [[1, C]], 128, -1, "imask")
     asel(T.ident[:], T.ones[:], [[-1, 128]], A.is_equal, 0, 1, "ones", "ident")
     for a in (0, 64):
         iota(T.io47[:, a:a + 64], [[32, 2], [0, 2], [1, 16]], 0, 0, "io47%d" % a, True)
     ts(T.cz[:, 0::4], T.io47[:], col("p47"), A.is_equal, "io470 io4764 c_p47 cz", "cz_")
     quant("qcz", T.cz[:], "cz cz_")
     hold[0] = False
-    act(T.cr[:, 0::4], T.pe[:], "pe", "cr_0")
-    act(T.cr[:, 1::4], T.pe[:], "pe", "cr_1")
-    act(T.cr[:, 2::4], T.po[:], "po", "cr_2", scale=0.5)
-    act(T.cr[:, 3::4], T.po[:], "po", "cr_3", scale=0.5)
-    act(T.cr5[:, 0::4], T.pe[:], "pe", "cr5")
-    act(T.cr5[:, 1::4], T.po[:], "po cr5", "cr5_")
+    def ones():
+        for c, k, n, w in (("cr", 0, "pe", 1.0), ("cr", 1, "pe", 1.0), ("cr", 2, "po", 0.5), ("cr", 3, "po", 0.5), ("cr5", 0, "pe", 1.0), ("cr5", 1, "po", 1.0)):
+            ts(T[c][:, k::4], T[n][:], w, A.mult, n + " cr5", "%s_%d" % (c, k))
+
     hold[0] = True
     op("v", "imask", "imask", lambda e: e.tensor_scalar(T.imask[:], T.imask[:], 15, None, A.bitwise_and))
     ts(T.mask[:], T.imask[:], 0.0, A.is_equal, "imask", "mask")
@@ -318,9 +331,10 @@ def rank_program(g, core, T, topo):
                              ("u1", 0.0, {3: -1, 11: 1, 13: -1}), ("u2", 0.0, {3: -1, 12: 1, 13: 1}), ("ug", 0.0, {3: -8}),
                              ("uo", 0.0, {3: 4, 11: 2, 12: 2, 13: 2})):
         if base:
-            act(om(n), om("re"), RE + " om", n, scale=base)
+            act(om(n), om("re"), RE + " om", n + "b", scale=base)
         for r, w in special.items():
-            act(om(n, r, 16), T[rel(r)][:, r::16], "om " + rel(r), n, scale=float(w))
+            act(om(n, r, 16), T[rel(r)][:, r::16], "om %s %sb" % (rel(r), n), "%s_%d" % (n, r), scale=float(w))
+        GRP[n] = " ".join(["om", n + "b"] + ["%s_%d" % (n, r) for r in special])
 
     def sum3(dst, keys, src, vn):
         for k in range(3):
@@ -407,7 +421,8 @@ def rank_program(g, core, T, topo):
     hold[0] = False
     for t in range(R):
         now, old = "%d" % (t % 2), "%d" % ((t + 1) % 2)
-        quant("qx", T.xt[:], "xt")
+        if t:
+            quant("qx", T.xt[:], "xt")
         for bank, la in ((5, 512), (6, 512), (4, 384), (1, 0), (2, 128), (3, 256)):
             mm(bank, "ua", "qx", True, True, la=la, lk="uac uas")
         op("v", "ps5", "tc", lambda e: e.transpose(T.tc[:], ps(5)))
@@ -425,16 +440,26 @@ def rank_program(g, core, T, topo):
                 act(nsw(k), ps(1 + k), "ps%d" % (1 + k), "ns%d" % k)
             act(T.srt[:], ps(1), "ps1", "srt")
             act(T.lrow[:], T.ioj[:].indirect(lks(0)), "ioj lk16", "lrow")
-        for b in range(10):
+        def sign(b):
+            so = 320 * (b % 2)
+            act(T.sg[:, so:so + 320], ps(6), "ps6 tc", "sg%d" % (b % 2), f=F.Sign, scale=-1.0, bias=T.tc[:, 32 * b:32 * b + 1])
+
+        sign(0)
+        lastw["rt4_3x"] = []
+        for b in range(9):
             e = 32 * b + 32
             sg, so = "sg%d" % (b % 2), 320 * (b % 2)
-            act(T.sg[:, so:so + 320], ps(6), "ps6 tc", sg, f=F.Sign, scale=-1.0, bias=T.tc[:, 32 * b:32 * b + 1])
+            if b < 8:
+                sign(b + 1)
             n, s = "rt%d" % (b // 2), 2 + b % 2
             act(T[n][:, s:4 * e:4], T.sg[:, so:so + e], sg, "%s_%d" % (n, s), f=F.Sign, scale=-1.0, bias=-0.5)
             if e < C:
                 act(T[n][:, 4 * e + s::4], T.sg[:, so + e:so + C], sg, "%s_%dx" % (n, s), f=F.Sign, scale=-1.0, bias=0.5)
             else:
                 lastw["%s_%dx" % (n, s)] = []
+        if t:
+            for k in range(3):
+                act(nsw(k), ps(1 + k), "ps%d" % (1 + k), "ns%d" % k)
         rk = 0
 
         def count(q, last=False):
@@ -444,9 +469,8 @@ def rank_program(g, core, T, topo):
                 keys = "rt5 rt5_0 " + " ".join("rt5_1%d" % a for a in range(4))
             d = ("ra_", "rb_")[q % 2]
             quant(d, T[n][:], keys)
-            mm(7, "qcr5" if q == 5 else "qcr", d, q == 0, q == 5)
+            mm(7, "qcr5" if q == 5 else "qcr", d, q == 0, q == 4)
 
-        tt(T.rt5[:, 0::4], T.eqe[:], T.tri[:], A.mult, "eqe tri rt5", "rt5_0")
         for b in range(10):
             e = 32 * b + 32
             n, s = "rt%d" % (b // 2), b % 2
@@ -458,17 +482,22 @@ def rank_program(g, core, T, topo):
                 lastw["%s_%dx" % (n, s)] = []
             if b in (5, 7, 9):
                 if t == 0 and b == 5:
+                    ones()
                     quant("qcr", T.cr[:], "cr_0 cr_1 cr_2 cr_3")
-                    quant("qcr5", T.cr5[:], "cr5 cr5_")
                 count(rk)
                 rk += 1
+        ts(T.rt4[:, 3::4], ps(5), T.tc[:, 288:289], A.is_gt, "ps5 tc", "rt4_3", 2.0, A.mult)
+        if t == 0:
+            quant("qcr5", T.cr5[:], "cr5 cr5_0 cr5_1")
+            bits()
+        tt(T.rt5[:, 0::4], T.eqe[:], T.tri[:], A.mult, "eqe tri rt5", "rt5_0")
         if t == 0:
             own = T.srt[:]
             for k in (1, 2):
                 for s, f in ((0, A.is_lt), (1, A.is_le)):
                     i = 2 * (k - 1) + s
-                    tt(T.flg[:, i::4], nsw(k).indirect(lks(k)), own, f, "srt ns%d lk16" % k, "flg")
-            quant("sq", T.flg[:], "flg")
+                    tt(T.flg[:, i::4], nsw(k).indirect(lks(k)), own, f, "srt ns%d lk16" % k, "flg%d" % i)
+            quant("sq", T.flg[:], "flg0 flg1 flg2 flg3")
             tt(T.lrow[:], T.lrow[:], T.ioj[:], A.is_lt, "lrow ioj", "lrow")
             tt(T.g1[:], nsw(0).indirect(lks(0)), own, A.is_le, "srt ns0 lk16", "g1")
             tt(T.g2[:], nsw(0).indirect(lks(0)), own, A.is_lt, "srt ns0 lk16", "g2")
@@ -476,9 +505,8 @@ def rank_program(g, core, T, topo):
             tt(T.kt[:, 0::4], T.g1[:], T.g2[:], A.max, "g1 g2 kt", "kt_0")
             quant("kq", T.kt[:], "kt kt_0")
             tt(T.gp[:, 1::4], T.tb[:], T.tb[:], A.is_equal, "tb gp", "gp_1")
-        while rk < 6:
-            count(rk)
-            rk += 1
+        for q in (3, 5, 4):
+            count(q)
         if t == 0:
             flush()
             mm(0, "qci1", "sq", True, False)
@@ -519,6 +547,7 @@ def rank_program(g, core, T, topo):
             table(u("lg"), "lg", T.srt[:, 0:64], "srt", n=64)
             for b in range(4):
                 act(T.et[:, b:256:4], T.fo[:, 320 * b:320 * b + 320].indirect(u("lg")), "lg et fo%d" % b, "et_%d" % b, scale=2.0)
+            act(T.g2[:], nsw(2).indirect(lks(2)), "ns2 lk16", "g2")
 
         @later(3)
         def _():
@@ -535,10 +564,8 @@ def rank_program(g, core, T, topo):
             tot["arr%d" % t] = 2 * ne
             tot["snt%d" % t] = 2 * ne
             lastw["aq%d" % t] = [("arr%d" % t, 2 * ne, {}, "dma")]
-            if t:
-                act(nsw(2), ps(3), "ps3", "ns2")
-                act(nsw(1), ps(2), "ps2", "ns1")
-            act(T.g2[:], nsw(2).indirect(lks(2)), "ns2 lk16", "g2")
+            act(T.g1[:], nsw(1).indirect(lks(1)), "ns1 lk16", "g1")
+            tt(T.pp[:, 3::4], nsw(1).indirect(lks(1)), T.g2[:], A.is_le, "ns1 lk16 g2 pp", "pp3")
 
         @later(2)
         def _():
@@ -548,13 +575,6 @@ def rank_program(g, core, T, topo):
                 routes_tables()
 
         @later(4)
-        def _():
-            tt(T.pp[:, 3::4], nsw(1).indirect(lks(1)), T.g2[:], A.is_le, "ns1 lk16 g2 pp", "pp3")
-            if t:
-                act(nsw(0), ps(1), "ps1", "ns0")
-            act(T.g1[:], nsw(1).indirect(lks(1)), "ns1 lk16", "g1")
-
-        @later(5)
         def _():
             tt(T.pp[:, 2::4], nsw(0).indirect(lks(0)), T.g2[:], A.is_le, "ns0 lk16 g2 pp", "pp2")
             tt(T.pp[:, 1::4], nsw(0).indirect(lks(0)), T.g1[:], A.is_le, "ns0 lk16 g1 pp", "pp1")
@@ -575,19 +595,20 @@ def rank_program(g, core, T, topo):
             act(T.st[:, 3::4], T.pub[:], "st pub", "st_3")
             cp(T.st[:, 2:64 * SPLIT:4], T.pub[:].indirect(lks(2, 0, SPLIT)), "st pub lk16", "st_2")
             act(T.st[:, 64 * SPLIT + 2::4], T.pub[:].indirect(lks(2, SPLIT, 20)), "st pub lk16", "st_2x")
-            quant("sq", T.st[:], "st st_0 st_1 st_2 st_2x st_3")
-            mm(0, "qcm", "sq", False, True)
-            for fn in ex[i]:
-                fn()
             if i == SWEEPS - 1:
                 mm(5, "qcbw", "gq" + now, True, False)
                 mm(5, "qcpw", "pq" + now, False, False)
+            quant("sq", T.st[:], "st st_0 st_1 st_2 st_2x st_3")
+            if i == SWEEPS - 1:
                 mm(5, "qcmw", "sq", False, True)
+                mm(6, "qckg", "gq" + now, True, False)
+            mm(0, "qcm", "sq", False, True)
+            for fn in ex[i]:
+                fn()
         act(T.kt[:, 1::4], ps(0), "ps0 kt", "kt_1")
         ts(T.kt[:, 0::4], ps(5), 0.0, A.max, "ps5 kt", "kt_0", 1.0, A.min)
         quant("kq", T.kt[:], "kt kt_0 kt_1")
-        mm(6, "qck", "kq", True, False)
-        mm(6, "qckg", "gq" + now, False, True)
+        mm(6, "qck", "kq", False, True)
         table(T.ki4[:, 0:20], "ki0", ps(6), "ps6")
         for a in range(1, 4):
             cp(T.ki4[:, 20 * a:20 * a + 20], T.sc[:, 15:C:16], "sc", "ki%d" % a)
@@ -605,14 +626,14 @@ def rank_program(g, core, T, topo):
         cp(u("dl4"), T.kd4[:, 0:80], "kd4c", "dl4")
         lastw["kd4"] = lastw["kd4c"]
         readers["kd4"] = list(readers.get("kd4c", []))
-        for a in (0, 1):
+        for a in (0, 1, 2):
             act(T.ds4[:, 640 * a:640 * a + 320], T.iot[:].indirect(u("dl4", 20 * a, 20 * a + 20)), "dl4 iot", "ds4%d" % a)
         tt(T.kd[:], T.kz[:], T.lwd[:], A.mult, "kz0 kz1 kz2 " + LWD, "kd")
         tt(T.dl[:], T.kd[:, 0:20], T.nat[:], A.add, "kd nat", "dl")
         tt(T.dl[:], T.dl[:], T.kd[:, 20:40], A.add, "dl kd", "dl")
         tt(T.dl[:], T.dl[:], T.kd[:, 40:60], A.add, "dl kd", "dl")
         cp(u("dl16"), T.dl[:], "dl", "dl16")
-        for a in (2, 3):
+        for a in (3,):
             cp(T.ds4[:, 640 * a:640 * a + 320], T.iot[:].indirect(u("dl4", 20 * a, 20 * a + 20)), "dl4 iot", "ds4%d" % a)
         DS = "ds40 ds41 ds42 ds43 ds4s "
 
@@ -628,14 +649,18 @@ def rank_program(g, core, T, topo):
         for n in ("c1", "c2", "e16"):
             table(u(n), n, T.ds4[:, 0:2240].indirect(u(cur)), DS + cur)
             cur = n
-        table(u("hl"), "hl", T.ds4[:, 320:2560].indirect(u("e16")), DS + "e16")
         if t == R - 1:
             act(T.lrow[:], T.num[:].indirect(u("e16")), "num e16", "lrow")
             act(T.ndr[:, 0:320], T.lrow[:], "lrow c_cl", "ndr_0", f=F.Identity, bias=col("cl"))
+        tt(T.mk[:], T.ds4[:, 320:2560].indirect(u("e16")), T.mask[:], A.mult, DS + "e16 mask", "mk")
         for b in range(4):
+            if b == 1:
+                op("v", "mk sc0", "sc", lambda e: e.tensor_tensor_scan(T.sc[:], T.sc0[:], T.mk[:], 0.0, A.mult, A.add))
+            if b == 2:
+                cp(u("hl"), T.sc[:, 15:C:16], "sc", "hl")
             tt(T.zz[:, 320 * b:320 * b + 320], fwin(b).indirect(u("e16")), T.zd[:, 320 * b:320 * b + 320], A.add, "e16 zd%d f4%d" % (b, b // 2), "zz%d" % b)
         for b in range(4):
-            tt(T.xt[:, b::4], T.h4[:, 80 * b:80 * b + 1040].indirect(u("hl")), T.zz[:, 320 * b:320 * b + 320], A.add, "hl h4 zz%d" % b, "xt")
+            tt(T.xt[:, b::4], T.h4[:, 80 * b:80 * b + 1040].indirect(u("hl")), T.zz[:, 320 * b:320 * b + 320], A.add, "hl h4 zz%d" % b, "xt%d" % b)
 
     quant("qx", T.xt[:], "xt")
     mm(1, "qv", "qx", True, True)

@@ -24,12 +24,12 @@ for _n, _w in (("xt", 1280), ("ut", 512), ("vt", 512), ("sga", 320), ("sgb", 320
                ("om", 128 * 23), ("ce", 2048), ("flg", 1280)):
     if _n not in ("sga", "sgb", "foa", "fob", "f4a", "f4b"):
         _s(_n, _w, BF)
-for _n, _w in (("sg", 640), ("fo", 1280), ("f4", 5120), ("zero", 1280), ("j31", 320), ("tri", 320), ("zt", 960), ("om", 1792)):
+for _n, _w in (("sg", 960), ("fo", 1280), ("f4", 5120), ("zero", 1280), ("j31", 320), ("tri", 320), ("zt", 960), ("om", 2560)):
     _s(_n, _w, BF)
 for _i in range(6):
     _s("rt%d" % _i, 1280, BF)
 CONSTS = ["cm", "cmw", "ci1", "ci2", "cb", "cbw", "cpw", "cs", "ck", "ckg", "cn2", "cr", "cr5", "cz"]
-OM = {_n: 128 * _i for _i, _n in enumerate([_x + _y for _x in "wu" for _y in "012go"] + ["tm0", "tm1", "tm2", "re"])}
+OM = {_n: 128 * _i for _i, _n in enumerate([_x + _y for _x in "wu" for _y in "012go"] + ["tm%d" % _y for _y in range(9)] + ["re"])}
 LOC = {"eb": ("qk", 0, 512)}
 for _i, _n in enumerate(CONSTS):
     _s(_n, 512, BF)
@@ -336,18 +336,25 @@ def rank_program(g, core, T, topo):
             act(om(n, r, 16), T[rel(r)][:, r::16], "om %s %sb" % (rel(r), n), "%s_%d" % (n, r), scale=float(w))
         GRP[n] = " ".join(["om", n + "b"] + ["%s_%d" % (n, r) for r in special])
 
-    def sum3(dst, keys, src, vn):
+    def sum3(dst, keys, src, vn, n):
         for k in range(3):
-            act(om("tm%d" % k), om("%s%d" % (src, k)), "%s%d kct" % (src, k), "tm%d" % k, scale=vec("%s%d" % (vn, k)))
-        tt(om("tm0"), om("tm0"), om("tm1"), A.add, "tm0 tm1", "tm0")
-        tt(dst, om("tm0"), om("tm2"), A.add, "tm0 tm2 " + keys.split("_")[0], keys)
+            act(om("tm%d" % (n + k)), om("%s%d" % (src, k)), "%s%d kct" % (src, k), "tm%d" % (n + k), scale=vec("%s%d" % (vn, k)))
+        x, y, z = ("tm%d" % (n + k) for k in range(3))
+        adds[0].append(lambda: tt(om(x), om(x), om(y), A.add, x + " " + y, x))
+        adds[1].append(lambda: tt(dst, om(x), om(z), A.add, x + " " + z + " " + keys.split("_")[0], keys))
+
+    adds = [[], [], []]
 
     for c, w in (("cm", "w"), ("cmw", "u")):
         for k in range(3):
             act(T[c][:, k::4], om("%s%d" % (w, k)), "%s%d kct" % (w, k), "%s_%d" % (c, k), scale=vec("g%d" % k))
-        sum3(T[c][:, 3::4], c + "_3", w, "x")
+        sum3(T[c][:, 3::4], c + "_3", w, "x", 0 if c == "cm" else 3)
+    sum3(T.cs[:, 1::4], "cs_", "w", "s", 6)
+    for fs in adds:
+        for fn in fs:
+            fn()
+    for c in ("cm", "cmw"):
         quant("q" + c, T[c][:], "%s_0 %s_1 %s_2 %s_3" % (c, c, c, c))
-    sum3(T.cs[:, 1::4], "cs_", "w", "s")
     quant("qcs", T.cs[:], "cs cs_")
     for n, bit in (("1", "b0"), ("2", "b2")):
         ts(col("le" + n), vec("i0"), 4.0, A.mult, "kct c_" + bit, "c_le" + n, col(bit), A.mult)
@@ -398,13 +405,13 @@ def rank_program(g, core, T, topo):
     LWD = "lwd0 lwd1 lwd2"
     LWD4 = " ".join("lwd4%d%d" % (k, a) for k in range(3) for a in range(4))
 
-    def table(out, ok, src, reads, n=C, add=None):
-        tt(T.mk[:, 0:n], src, T.mask[:, 0:n], A.mult, reads + " mask", "mk")
+    def scan(n):
         op("v", "mk sc0", "sc", lambda e: e.tensor_tensor_scan(T.sc[:, 0:n], T.sc0[:, 0:n], T.mk[:, 0:n], 0.0, A.mult, A.add))
-        if add is None:
-            cp(out, T.sc[:, 15:n:16], "sc", ok)
-        else:
-            ts(out, T.sc[:, 15:n:16], add[0], A.add, "sc " + add[1], ok)
+
+    def table(out, ok, src, reads, n=C):
+        tt(T.mk[:, 0:n], src, T.mask[:, 0:n], A.mult, reads + " mask", "mk")
+        scan(n)
+        cp(out, T.sc[:, 15:n:16], "sc", ok)
 
     def spread4(dst, src, w, do=0, so=0, pitch=None):
         m = []
@@ -441,14 +448,14 @@ def rank_program(g, core, T, topo):
             act(T.srt[:], ps(1), "ps1", "srt")
             act(T.lrow[:], T.ioj[:].indirect(lks(0)), "ioj lk16", "lrow")
         def sign(b):
-            so = 320 * (b % 2)
-            act(T.sg[:, so:so + 320], ps(6), "ps6 tc", "sg%d" % (b % 2), f=F.Sign, scale=-1.0, bias=T.tc[:, 32 * b:32 * b + 1])
+            so = 320 * (b % 3)
+            act(T.sg[:, so:so + 320], ps(6), "ps6 tc", "sg%d" % (b % 3), f=F.Sign, scale=-1.0, bias=T.tc[:, 32 * b:32 * b + 1])
 
         sign(0)
         lastw["rt4_3x"] = []
         for b in range(9):
             e = 32 * b + 32
-            sg, so = "sg%d" % (b % 2), 320 * (b % 2)
+            sg, so = "sg%d" % (b % 3), 320 * (b % 3)
             if b < 8:
                 sign(b + 1)
             n, s = "rt%d" % (b // 2), 2 + b % 2
@@ -457,9 +464,6 @@ def rank_program(g, core, T, topo):
                 act(T[n][:, 4 * e + s::4], T.sg[:, so + e:so + C], sg, "%s_%dx" % (n, s), f=F.Sign, scale=-1.0, bias=0.5)
             else:
                 lastw["%s_%dx" % (n, s)] = []
-        if t:
-            for k in range(3):
-                act(nsw(k), ps(1 + k), "ps%d" % (1 + k), "ns%d" % k)
         rk = 0
 
         def count(q, last=False):
@@ -469,7 +473,7 @@ def rank_program(g, core, T, topo):
                 keys = "rt5 rt5_0 " + " ".join("rt5_1%d" % a for a in range(4))
             d = ("ra_", "rb_")[q % 2]
             quant(d, T[n][:], keys)
-            mm(7, "qcr5" if q == 5 else "qcr", d, q == 0, q == 4)
+            mm(7, "qcr5" if q == 5 else "qcr", d, q == 0, q == 5)
 
         for b in range(10):
             e = 32 * b + 32
@@ -505,8 +509,22 @@ def rank_program(g, core, T, topo):
             tt(T.kt[:, 0::4], T.g1[:], T.g2[:], A.max, "g1 g2 kt", "kt_0")
             quant("kq", T.kt[:], "kt kt_0")
             tt(T.gp[:, 1::4], T.tb[:], T.tb[:], A.is_equal, "tb gp", "gp_1")
-        for q in (3, 5, 4):
+        def unpack(b):
+            bank = (4, 5, 6, 4)[b]
+            mm(bank, "eb", "qx", True, True, la=128 * b)
+            act(T.fo[:, 320 * b:320 * b + 320], ps(bank), "ps%d" % bank, "fo%d" % b)
+            if b % 2:
+                dma(spread4(T.f4, T.fo, 640, do=1280 * (b - 1), so=320 * (b - 1)), "fd%d" % t, "fo%d fo%d" % (b - 1, b), "f4%d" % (b // 2))
+
+        late = []
+        for q in (3, 4, 5):
             count(q)
+        if t:
+            for b in range(3):
+                unpack(b)
+            late.append(unpack)
+            for k in (2, 1, 0):
+                act(nsw(k), ps(1 + k), "ps%d" % (1 + k), "ns%d" % k)
         if t == 0:
             flush()
             mm(0, "qci1", "sq", True, False)
@@ -516,13 +534,8 @@ def rank_program(g, core, T, topo):
         if t:
             mm(0, "qcs", "kq", True, False)
         mm(0, "qcb", "gq" + now, False, True)
-        def unpack(b):
-            bank = (4, 5, 6, 4)[b]
-            mm(bank, "eb", "qx", True, True, la=128 * b)
-            act(T.fo[:, 320 * b:320 * b + 320], ps(bank), "ps%d" % bank, "fo%d" % b)
-            if b % 2:
-                dma(spread4(T.f4, T.fo, 640, do=1280 * (b - 1), so=320 * (b - 1)), "fd%d" % t, "fo%d fo%d" % (b - 1, b), "f4%d" % (b // 2))
-
+        for fn in late:
+            fn(3)
         ex = {i: [] for i in range(6)}
 
         def later(i):
@@ -532,22 +545,40 @@ def rank_program(g, core, T, topo):
 
         @later(0)
         def _():
-            table(u("rw"), "rw", ps(7), "ps7", add=(col("off"), "c_off"))
-            unpack(0)
-            unpack(1)
+            scan(C)
+            ts(T.sl[:], ps(7), col("s1"), A.add, "ps7 c_s1 c_s2", "sl", col("s2"), A.min)
+            dma(spread4(T.ds4, T.sl, 320, do=320, pitch=640), "dd%d" % t, "sl", "ds4s")
+            if t == 0:
+                unpack(0)
+                unpack(1)
+            else:
+                act(T.g2[:], nsw(2).indirect(lks(2)), "ns2 lk16", "g2")
+
+        tt(T.mk[:], ps(7), T.mask[:], A.mult, "ps7 mask", "mk")
+
+        def ready():
+            ts(u("rw"), T.sc[:, 15:C:16], col("off"), A.add, "sc c_off", "rw")
 
         @later(1)
         def _():
             op("v", "rw ioj", "srt", lambda e: e.tensor_copy(T.srt[:].indirect(u("rw")), T.ioj[:]))
-            unpack(2)
-            unpack(3)
+            if t == 0:
+                unpack(2)
+                unpack(3)
+                act(T.g2[:], nsw(2).indirect(lks(2)), "ns2 lk16", "g2")
+            else:
+                act(T.g1[:], nsw(1).indirect(lks(1)), "ns1 lk16", "g1")
 
         @later(2)
         def _():
-            table(u("lg"), "lg", T.srt[:, 0:64], "srt", n=64)
+            tt(T.mk[:, 0:64], T.srt[:, 0:64], T.mask[:, 0:64], A.mult, "srt mask", "mk")
+            tt(T.pp[:, 2::4], nsw(0).indirect(lks(0)), T.g2[:], A.is_le, "ns0 lk16 g2 pp", "pp2")
+            scan(64)
+            cp(u("lg"), T.sc[:, 15:64:16], "sc", "lg")
             for b in range(4):
                 act(T.et[:, b:256:4], T.fo[:, 320 * b:320 * b + 320].indirect(u("lg")), "lg et fo%d" % b, "et_%d" % b, scale=2.0)
-            act(T.g2[:], nsw(2).indirect(lks(2)), "ns2 lk16", "g2")
+            if t == 0:
+                act(T.g1[:], nsw(1).indirect(lks(1)), "ns1 lk16", "g1")
 
         @later(3)
         def _():
@@ -564,19 +595,15 @@ def rank_program(g, core, T, topo):
             tot["arr%d" % t] = 2 * ne
             tot["snt%d" % t] = 2 * ne
             lastw["aq%d" % t] = [("arr%d" % t, 2 * ne, {}, "dma")]
-            act(T.g1[:], nsw(1).indirect(lks(1)), "ns1 lk16", "g1")
             tt(T.pp[:, 3::4], nsw(1).indirect(lks(1)), T.g2[:], A.is_le, "ns1 lk16 g2 pp", "pp3")
 
         @later(2)
         def _():
-            ts(T.sl[:], ps(7), col("s1"), A.add, "ps7 c_s1 c_s2", "sl", col("s2"), A.min)
-            dma(spread4(T.ds4, T.sl, 320, do=320, pitch=640), "dd%d" % t, "sl", "ds4s")
             if t == 0:
                 routes_tables()
 
         @later(4)
         def _():
-            tt(T.pp[:, 2::4], nsw(0).indirect(lks(0)), T.g2[:], A.is_le, "ns0 lk16 g2 pp", "pp2")
             tt(T.pp[:, 1::4], nsw(0).indirect(lks(0)), T.g1[:], A.is_le, "ns0 lk16 g1 pp", "pp1")
             quant("pq" + now, T.pp[:], "pp pp1 pp2 pp3")
 
@@ -590,6 +617,8 @@ def rank_program(g, core, T, topo):
         for i in range(SWEEPS):
             ts(T.pub[:], ps(0), vec("lo"), A.max, "ps0 kct", "pub", vec("hi"), A.min)
             mm(0, "qcb", "gq" + now, True, False)
+            if i == 1:
+                ready()
             act(T.st[:, 0::4], T.pub[:].indirect(lks(0)), "st pub lk16", "st_0")
             cp(T.st[:, 1::4], T.pub[:].indirect(lks(1)), "st pub lk16", "st_1")
             act(T.st[:, 3::4], T.pub[:], "st pub", "st_3")
@@ -619,21 +648,21 @@ def rank_program(g, core, T, topo):
         mm(5, "qcz", "zq", True, True, n=240)
         for k in range(3):
             tt(T.kz[:, 20 * k:20 * k + 20], T.kb4[:, 80 * k:80 * k + 20], T.kcst[:, 20 * k:20 * k + 20], A.is_equal, "kb%d kcst" % k, "kz%d" % k)
+        tt(T.kd[:], T.kz[:], T.lwd[:], A.mult, "kz0 kz1 kz2 " + LWD, "kd")
         tt(T.kd4[:], ps(5, 0, 240), T.lwd4[:], A.mult, "ps5 " + LWD4, "kd4")
+        tt(T.dl[:], T.kd[:, 0:20], T.nat[:], A.add, "kd nat", "dl")
         tt(T.kd4[:, 0:80], T.kd4[:, 0:80], T.nat4[:], A.add, "kd4 nat4", "kd4a")
         tt(T.kd4[:, 80:160], T.kd4[:, 80:160], T.kd4[:, 160:240], A.add, "kd4", "kd4b")
+        tt(T.dl[:], T.dl[:], T.kd[:, 20:40], A.add, "dl kd", "dl")
         tt(T.kd4[:, 0:80], T.kd4[:, 0:80], T.kd4[:, 80:160], A.add, "kd4a kd4b", "kd4c")
+        tt(T.dl[:], T.dl[:], T.kd[:, 40:60], A.add, "dl kd", "dl")
         cp(u("dl4"), T.kd4[:, 0:80], "kd4c", "dl4")
+        cp(u("dl16"), T.dl[:], "dl", "dl16")
         lastw["kd4"] = lastw["kd4c"]
         readers["kd4"] = list(readers.get("kd4c", []))
-        for a in (0, 1, 2):
+        for a in (0, 1):
             act(T.ds4[:, 640 * a:640 * a + 320], T.iot[:].indirect(u("dl4", 20 * a, 20 * a + 20)), "dl4 iot", "ds4%d" % a)
-        tt(T.kd[:], T.kz[:], T.lwd[:], A.mult, "kz0 kz1 kz2 " + LWD, "kd")
-        tt(T.dl[:], T.kd[:, 0:20], T.nat[:], A.add, "kd nat", "dl")
-        tt(T.dl[:], T.dl[:], T.kd[:, 20:40], A.add, "dl kd", "dl")
-        tt(T.dl[:], T.dl[:], T.kd[:, 40:60], A.add, "dl kd", "dl")
-        cp(u("dl16"), T.dl[:], "dl", "dl16")
-        for a in (3,):
+        for a in (2, 3):
             cp(T.ds4[:, 640 * a:640 * a + 320], T.iot[:].indirect(u("dl4", 20 * a, 20 * a + 20)), "dl4 iot", "ds4%d" % a)
         DS = "ds40 ds41 ds42 ds43 ds4s "
 

from concourse.bass import DstId, RemoteDMATransfer
from concourse.mybir import dt, AluOpType as A, ActivationFunctionType as F

C, GW, R, SWEEPS = 320, 64, 3, 6
BF, F32, I32, U16, X4, U8 = "bfloat16", "float32", "int32", "uint16", "float8_e4m3fn_x4", "uint8"
SPLIT = 18

SCRATCH = {}


def _s(n, w, d):
    SCRATCH[n] = ("sbuf", [128, w], d)


def _q(n, w):
    _s(n + "c", w, X4)
    _s(n + "s", w, U8)


for _n, _w in (("xt", 1280), ("ut", 512), ("vt", 512), ("sga", 320), ("sgb", 320), ("gp", 1280), ("pp", 1280), ("st", 1280),
               ("pub", 320), ("kt", 1280), ("eqe", 320), ("eqo", 320), ("et", 512), ("zero", 512), ("foa", 640), ("fob", 640),
               ("f4a", 2560), ("f4b", 2560), ("ho", 320), ("h4", 1280), ("zd", 1280), ("zz", 1280), ("ident", 128),
               ("ones", 128), ("ra", 128), ("rb", 128), ("pe", 128), ("po", 128), ("rel0", 128), ("rel1", 128), ("rel4", 128),
               ("om", 128 * 23), ("ce", 2048), ("flg", 1280)):
    if _n not in ("sga", "sgb", "foa", "fob", "f4a", "f4b"):
        _s(_n, _w, BF)
for _n, _w in (("sg", 960), ("fo", 1280), ("f4", 5120), ("zero", 1280), ("j31", 320), ("tri", 320), ("zt", 960), ("om", 2560)):
    _s(_n, _w, BF)
for _i in range(6):
    _s("rt%d" % _i, 1280, BF)
CONSTS = ["cm", "cmw", "ci1", "ci2", "cb", "cbw", "cpw", "cs", "ck", "ckg", "cn2", "cr", "cr5", "cz"]
OM = {_n: 128 * _i for _i, _n in enumerate([_x + _y for _x in "wu" for _y in "012go"] + ["tm%d" % _y for _y in range(9)] + ["re"])}
LOC = {"eb": ("qk", 0, 512)}
for _i, _n in enumerate(CONSTS):
    _s(_n, 512, BF)
    LOC["q" + _n] = ("qk", 512 + 128 * _i, 128)
_q("qk", 512 + 128 * len(CONSTS))
for _i, _n in enumerate(("gq0", "gq1", "pq0", "pq1", "ra_", "rb_", "sq", "kq")):
    LOC[_n] = ("qf", 320 * _i, 320)
LOC["zq"] = ("qf", 2560, 240)
_q("qf", 2800)
for _i in range(R):
    LOC["qe%d" % _i] = ("qe", 128 * _i, 128)
_q("qe", 128 * R)
for _n, _w in (("ns", 960), ("tb", 320), ("tc", 320), ("mk", 320), ("sc", 320), ("srt", 320), ("ds4", 2560),
               ("iot", 2560), ("num", 2560), ("mask", 320), ("sc0", 320), ("ioj", 320), ("lwd", 60), ("kz", 60), ("kd", 60),
               ("dl", 20), ("nat", 20), ("io47", 128), ("lwd4", 240), ("nat4", 80), ("kd4", 240), ("sl", 320), ("cols", 32), ("kc0", 448), ("kct", 448), ("g1", 320), ("g2", 320),
               ("ndr", 640), ("ysb", 320), ("lrow", 320)):
    _s(_n, _w, F32)
for _n, _w in (("lki", 60), ("lk4", 240), ("ki4", 80), ("kb4", 240), ("kc4", 240), ("kcst", 60), ("ip", 1), ("ib", 8), ("inat", 20), ("imask", 320), ("iu", 40)):
    _s(_n, _w, I32)
OFS = {"dl16": (0, 20), "c1": (20, 20), "c2": (40, 20), "e16": (60, 20), "hl": (80, 20), "rw": (100, 20), "lg": (120, 4), "dl4": (124, 80)}
for _n, _w in (("lk16", 60), ("of", 204), ("ul", 40)):
    _s(_n, _w, U16)
for _n, _w in (("qu", 128), ("ua", 640), ("qv", 128), ("qw", 512), ("qx", 320)):
    _q(_n, _w)
for _i in range(R):
    _q("aq%d" % _i, 192)
for _i in range(8):
    SCRATCH["ps%d" % _i] = ("psum", [128, 512], F32)

SEMAPHORES = ["sv", "ss", "st_", "sg_", "zf1", "zf2", "zf3", "ldl4", "ldx", "ldu", "ldv", "ldw", "ldl", "ndo", "yo", "oco"]
for _i in range(R):
    SEMAPHORES += ["fd%d" % _i, "dd%d" % _i, "hd%d" % _i, "arr%d" % _i, "snt%d" % _i]


def rank_program(g, core, T, topo):
    rank = T.rank_of(core)
    if rank is None:
        return
    nxt = T.cores[(rank + 1) % len(T.cores)]
    ENG = {"v": g.vector, "s": g.scalar, "t": g.tensor, "g": g, "y": g.sync}
    CS = {"v": "sv", "s": "ss", "t": "st_", "g": "sg_"}
    tot, know, lastw, readers = {}, {q: {} for q in ENG}, {}, {}
    dmasem = set()
    GRP = {"xt": "xt xt0 xt1 xt2 xt3"}
    hold, pending = [False], []

    def flush():
        hold[0] = False
        for x in pending:
            op(*x)
        pending.clear()


    def settle(q, toks):
        want = {}
        for sem, val, clk, e in toks:
            if sem in dmasem:
                val = tot[sem]
            if sem not in want or want[sem][0] < val:
                want[sem] = (val, clk)
        k = know[q]
        for sem in sorted(want):
            val, clk = want[sem]
            if k.get(sem, 0) < val:
                ENG[q].wait_ge(T.sem[sem], val)
                for a, b in clk.items():
                    if k.get(a, 0) < b:
                        k[a] = b
                k[sem] = val

    def deps(q, reads, writes, dma):
        toks = []
        for r in reads:
            toks += lastw.get(r, [])
            if r[:2] == "ps" and r[2:].isdigit():
                toks += [x for x in readers.get(r, []) if x[3] != q]
        for w in writes:
            toks += [x for x in lastw.get(w, []) if dma or x[3] != q or q != "t"]
            toks += readers.get(w, [])
        return toks

    def done(tok, reads, writes):
        for r in reads:
            if r not in writes:
                readers.setdefault(r, []).append(tok)
        for w in writes:
            lastw[w] = [tok]
            readers[w] = []

    def op(q, reads, writes, fn):
        if hold[0] and q != "g":
            pending.append((q, reads, writes, fn))
            return
        reads = " ".join(GRP.get(x, x) for x in reads.split())
        reads, writes = reads.split(), writes.split()
        sem = CS[q]
        pool = [(sem, tot[sem], {}, q)] if q == "g" and sem in tot else []
        settle(q, deps(q, reads, writes, False) + pool)
        fn(ENG[q]).then_inc(T.sem[sem], 1)
        tot[sem] = tot.get(sem, 0) + 1
        clk = dict(know[q])
        clk[sem] = tot[sem]
        done((sem, tot[sem], clk, q), reads, writes)

    def dma(moves, sem, reads, writes):
        reads, writes = reads.split(), writes.split()
        dmasem.add(sem)
        toks = deps("", reads, writes, True)
        qs = []
        for q, o, i in moves:
            if q not in qs:
                qs.append(q)
                settle(q, toks)
            ENG[q].dma_start(o, i).then_inc(T.sem[sem], 16)
            tot[sem] = tot.get(sem, 0) + 16
        clk = {}
        for q in qs:
            for a, b in know[q].items():
                clk[a] = max(clk.get(a, 0), b)
        clk[sem] = tot[sem]
        done((sem, tot[sem], clk, "dma"), reads, writes)

    def ts(o, i, s1, o1, reads, writes, s2=None, o2=None, q="v"):
        if o2 is None:
            op(q, reads, writes, lambda e: e.tensor_scalar(o, i, s1, None, o1))
        else:
            op(q, reads, writes, lambda e: e.tensor_scalar(o, i, s1, s2, o1, o2))

    def tt(o, a, b, f, reads, writes):
        op("v", reads, writes, lambda e: e.tensor_tensor(o, a, b, f))

    def cp(o, i, reads, writes):
        op("v", reads, writes, lambda e: e.tensor_copy(o, i))

    def act(o, i, reads, writes, f=F.Copy, **kw):
        op("s", reads, writes, lambda e: e.activation(o, i, f, **kw))

    def fill(o, v, writes):
        op("v", "", writes, lambda e: e.memset(o, v))

    def quant(n, tile, tkeys, k=None, a=0, b=None):
        n2, o, w = LOC.get(n, (n, 0, None))
        c, s = T[n2 + "c"], T[n2 + "s"]
        b = b if b is not None else w or c.shape[1]
        a, b = a + o, b + o
        op("v", tkeys, k or n, lambda e: e.quantize_mx(c[:, a:b], s[:, a:b], tile))

    def mm(bank, l, r, start, stop, la=0, ra=0, n=C, lk=None, rk=None):
        p = T["ps%d" % bank]
        l2, lo, _w = LOC.get(l, (l, 0, 0))
        r2, ro, _w = LOC.get(r, (r, 0, 0))
        x, y = la + lo, ra + ro
        op("t", (lk or l) + " " + (rk or r), "ps%d" % bank, lambda e: e.matmul_mx(
            p[:, 0:n], T[l2 + "c"][:, x:x + 128], T[l2 + "s"][:, x:x + 128], T[r2 + "c"][:, y:y + n], T[r2 + "s"][:, y:y + n], start, stop))

    def ps(i, a=0, b=C):
        return T["ps%d" % i][:, a:b]

    def om(n, a=0, st=1):
        return T.om[:, OM[n] + a:OM[n] + 128:st]

    def u(n, a=0, b=None):
        o, w = OFS[n]
        return T.of[:, o + a:o + (w if b is None else b)]

    def lks(k, a=0, b=20):
        return T.lk16[:, 20 * k + a:20 * k + b]

    dma([("s", T.ut[:], T.u[:])], "ldu", "", "ut")
    dma([("y", T.xt[:], T.x[:])], "ldx", "", "xt")
    dma([("s", T.lki[:], T.lk[:])], "ldl", "", "lki")
    fill(T.ones[:], 1.0, "ones")
    fill(T.zero[:], 0.0, "zero")
    fill(T.cr5[:], 0.0, "cr5")
    fill(T.rt5[:], 0.0, "rt5")

    def zeros(sem, names):
        dma([("y", T[n][:, a:min(a + 1280, w)], T.zero[:, 0:min(1280, w - a)]) for n in names.split() for w in [SCRATCH[n][1][1]]
             for a in range(0, w, 1280)], sem, "zero", names)

    zeros("zf1", "om ce")
    zeros("zf2", "ci2 gp kt cb")
    zeros("zf3", "cs cbw cpw ck ckg cn2 cz pp et ho zt")
    dma([("y", T.qwc[:].bitcast(dt.uint8), T.wc[:]), ("y", T.qws[:], T.ws[:])], "ldw", "", "qw")
    L4 = []
    for h in range(8):
        for d in (h, h ^ 1, h ^ 4, h ^ 5):
            a = (h & 1) + 2 * (h >> 2)
            L4.append(("y", T.lk4[16 * d:16 * d + 16, 60 * a:60 * a + 60], T.lki[16 * h:16 * h + 16, :]))
    dma(L4, "ldl4", "lki", "lk4")
    dma([("y", T.vt[:], T.v[:])], "ldv", "", "vt")

    def iota(o, pat, base, ch, w, fl=False):
        if fl:
            op("g", "", w, lambda e: e.iota(o, pat, base, ch, allow_small_or_imprecise_dtypes=True))
        else:
            op("g", "", w, lambda e: e.iota(o, pat, base, ch))

    def asel(o, i, pat, cmp, base, ch, r, w):
        op("g", r, w, lambda e: e.affine_select(o, i, pat, cmp, 0.0, base, ch))

    for k, pat in enumerate(([[16, 8]], [[32, 4], [-16, 2]], [[-64, 2], [16, 4]], [[32, 4], [0, 2]], [[32, 4], [0, 2]])):
        iota(T.iu[:, 8 * k:8 * k + 8], pat, (0, 16, 64, 0, 16)[k], 0, "iu%d" % k)
    iota(T.ip[:], [[0, 1]], 0, 1, "ip")
    asel(T.ra[:], T.ones[:], [[-32, 4], [0, 32]], A.is_ge, 0, 1, "ones", "ra")
    asel(T.rb[:], T.ra[:], [[32, 4], [0, 32]], A.is_ge, 31, -1, "ra", "rb")
    asel(T.pe[:], T.rb[:], [[0, 4], [1, 2], [0, 16]], A.is_equal, 0, 0, "rb", "pe")
    asel(T.po[:], T.rb[:], [[0, 4], [1, 2], [0, 16]], A.not_equal, 0, 0, "rb", "po")
    iota(T.ioj[:], [[1, C]], 0, 0, "ioj", True)
    iota(T.inat[:], [[16, 20]], 0, 0, "inat")
    cp(T.ul[:], T.iu[:], "iu0 iu1 iu2 iu3 iu4", "ul")
    quant("qu", T.ut[:], "ut")
    op("v", "qu ul", "uac", lambda e: e.tensor_copy(T.uac[:].bitcast(dt.uint32), T.quc[:].bitcast(dt.uint32).indirect(T.ul[:, 0:40])))
    op("s", "qu ul", "uas", lambda e: e.activation(T.uas[:], T.qus[:].indirect(T.ul[:, 0:40]), F.Copy))
    cl = {}

    def col(name):
        cl.setdefault(name, len(cl))
        return T.cols[:, cl[name]:cl[name] + 1]

    quant("qx", T.xt[:], "xt")
    cp(T.lk16[:], T.lki[:], "lki", "lk16")
    iota(T.j31[:], [[0, 10], [1, 32]], 0, 0, "j31", True)

    def bits():
        for i, (sh, an) in enumerate(((4, 1), (5, 1), (6, 1), (0, 15))):
            op("v", "ip", "ib%d" % i, lambda e: e.tensor_scalar(T.ib[:, i:i + 1], T.ip[:], sh, an, A.logical_shift_right, A.bitwise_and))
        for i in range(4):
            cp(col("b%d" % i), T.ib[:, i:i + 1], "ib%d" % i, "c_b%d" % i)
        ts(col("p31"), col("b0"), 16.0, A.mult, "c_b0 c_b3", "c_p31", col("b3"), A.add)
        ts(T.tri[:], T.j31[:], col("p31"), A.is_gt, "j31 c_p31", "tri")

    hold[0] = True
    ts(col("a640"), col("b2"), 2.0, A.mult, "c_b2 c_b0", "c_a2", col("b0"), A.add)
    ts(col("off"), col("b0"), 144.0, A.mult, "c_b0", "c_off")
    ts(col("t63"), col("b0"), -144.0, A.mult, "c_b0", "c_t63", 63.5, A.add)
    ts(col("s1"), col("a640"), 320.0, A.mult, "c_a2 c_off", "c_s1", col("off"), A.add)
    ts(col("s2"), col("a640"), 320.0, A.mult, "c_a2", "c_s2", 64.0, A.add)
    ts(col("m1"), col("b0"), -1280.0, A.mult, "c_b0", "c_m1", 640.0, A.add)
    ts(col("m2"), col("b2"), -2560.0, A.mult, "c_b2", "c_m2", 1280.0, A.add)
    ts(col("cl"), col("b1"), 640.0, A.mult, "c_b1", "c_cl")
    ts(col("oa"), col("a640"), 640.0, A.mult, "c_a2 c_b3", "c_oa", col("b3"), A.add)
    for a in range(4):
        ts(col("n%d" % a), col("a640"), float(a), A.not_equal, "c_a2", "c_n%d" % a, 100.0, A.mult)
    ts(col("p47"), col("b1"), 32.0, A.mult, "c_b1 c_b3", "c_p47", col("b3"), A.add)
    fill(T.kc0[:], 0.0, "kc0")
    VEC = {"g0": {0: -3, 3: -3, 4: 3}, "g1": {5: -3, 6: -3, 7: 3}, "g2": {8: -3, 9: -3, 10: 3}, "x0": {0: 5, 3: 3, 4: -4, 11: 1},
           "x1": {1: 5, 3: 3, 4: -4, 12: 1}, "x2": {2: 5, 3: 3, 4: -4, 13: 1}, "i0": {0: 1}, "kv": {11: 1, 12: 2, 13: 4, 3: 8},
           "bb": {11: 1, 12: 2, 13: 4}, "s0": {11: 1}, "s1": {12: 1}, "s2": {13: 1}, "lo": {11: -99, 12: -99, 13: -99}, "hi": {11: 99, 12: 99, 13: 99}}
    KC = []

    def put(o, v, over, key):
        op("v", over, key, lambda e: e.memset(o, v))

    vi = {n: i for i, n in enumerate(VEC)}
    fill(T.kc0[:, 32 * vi["hi"]:32 * vi["hi"] + 32], 1.0, "kc0")
    for n, d in VEC.items():
        o = 32 * vi[n]
        for r, w in d.items():
            put(T.kc0[:, o + r:o + 32:16], float(w), "kc0", "kc0_%d" % (o + r))
            KC.append("kc0_%d" % (o + r))
    op("v", "kc0 " + " ".join(KC), "kct", lambda e: e.transpose(T.kct[:], T.kc0[:]))

    def vec(n):
        return T.kct[:, 32 * vi[n]:32 * vi[n] + 1]

    for n, p1, b1, p2, b2 in (("rel0", [[-16, 8], [0, 16]], 0, [[16, 8], [0, 16]], 15),
                              ("rel1", [[-32, 4], [16, 2], [0, 16]], -16, [[32, 4], [-16, 2], [0, 16]], 31),
                              ("rel4", [[64, 2], [-16, 4], [0, 16]], -64, [[-64, 2], [16, 4], [0, 16]], 79)):
        asel(T.ra[:], T.ones[:], p1, A.is_ge, b1, 1, "ones", "ra")
        asel(T[n][:], T.ra[:], p2, A.is_ge, b2, -1, "ra", n)
    iota(T.imask[:], [[1, C]], 128, -1, "imask")
    asel(T.ident[:], T.ones[:], [[-1, 128]], A.is_equal, 0, 1, "ones", "ident")
    for a in (0, 64):
        iota(T.io47[:, a:a + 64], [[32, 2], [0, 2], [1, 16]], 0, 0, "io47%d" % a, True)
    ts(T.cz[:, 0::4], T.io47[:], col("p47"), A.is_equal, "io470 io4764 c_p47 cz", "cz_")
    quant("qcz", T.cz[:], "cz cz_")
    hold[0] = False
    def ones():
        for c, k, n, w in (("cr", 0, "pe", 1.0), ("cr", 1, "pe", 1.0), ("cr", 2, "po", 0.5), ("cr", 3, "po", 0.5), ("cr5", 0, "pe", 1.0), ("cr5", 1, "po", 1.0)):
            ts(T[c][:, k::4], T[n][:], w, A.mult, n + " cr5", "%s_%d" % (c, k))

    hold[0] = True
    op("v", "imask", "imask", lambda e: e.tensor_scalar(T.imask[:], T.imask[:], 15, None, A.bitwise_and))
    ts(T.mask[:], T.imask[:], 0.0, A.is_equal, "imask", "mask")
    fill(T.sc0[:], 1.0, "sc0")
    fill(T.sc0[:, 0:C:16], 0.0, "sc0")
    for b in range(4):
        act(T.ce[:, 512 * b + b:512 * b + 512:4], T.ident[:], "ident ce", "ce_%d" % b, scale=0.5)
    quant("eb", T.ce[:], "ce ce_0 ce_1 ce_2 ce_3")
    def rel(r):
        return "rel0" if r < 5 or r > 10 else "rel1" if r < 8 else "rel4"

    for r in range(11):
        act(om("re", r, 16), T[rel(r)][:, r::16], "om " + rel(r), "re%d" % r)
    RE = " ".join("re%d" % r for r in range(11))
    for n, base, special in (("w0", -1.0, {0: -4, 11: 1}), ("w1", -1.0, {1: -4, 5: -4, 12: 1}), ("w2", -1.0, {2: -4, 8: -4, 13: 1}),
                             ("wg", -8.0, {}), ("wo", 4.0, {4: 3, 7: 3, 10: 3}), ("u0", 0.0, {3: -1, 11: -1, 12: -1}),
                             ("u1", 0.0, {3: -1, 11: 1, 13: -1}), ("u2", 0.0, {3: -1, 12: 1, 13: 1}), ("ug", 0.0, {3: -8}),
                             ("uo", 0.0, {3: 4, 11: 2, 12: 2, 13: 2})):
        if base:
            act(om(n), om("re"), RE + " om", n + "b", scale=base)
        for r, w in special.items():
            act(om(n, r, 16), T[rel(r)][:, r::16], "om %s %sb" % (rel(r), n), "%s_%d" % (n, r), scale=float(w))
        GRP[n] = " ".join(["om", n + "b"] + ["%s_%d" % (n, r) for r in special])

    def sum3(dst, keys, src, vn, n):
        for k in range(3):
            act(om("tm%d" % (n + k)), om("%s%d" % (src, k)), "%s%d kct" % (src, k), "tm%d" % (n + k), scale=vec("%s%d" % (vn, k)))
        x, y, z = ("tm%d" % (n + k) for k in range(3))
        adds[0].append(lambda: tt(om(x), om(x), om(y), A.add, x + " " + y, x))
        adds[1].append(lambda: tt(dst, om(x), om(z), A.add, x + " " + z + " " + keys.split("_")[0], keys))

    adds = [[], [], []]

    for c, w in (("cm", "w"), ("cmw", "u")):
        for k in range(3):
            act(T[c][:, k::4], om("%s%d" % (w, k)), "%s%d kct" % (w, k), "%s_%d" % (c, k), scale=vec("g%d" % k))
        sum3(T[c][:, 3::4], c + "_3", w, "x", 0 if c == "cm" else 3)
    sum3(T.cs[:, 1::4], "cs_", "w", "s", 6)
    for fs in adds:
        for fn in fs:
            fn()
    for c in ("cm", "cmw"):
        quant("q" + c, T[c][:], "%s_0 %s_1 %s_2 %s_3" % (c, c, c, c))
    quant("qcs", T.cs[:], "cs cs_")
    for n, bit in (("1", "b0"), ("2", "b2")):
        ts(col("le" + n), vec("i0"), 4.0, A.mult, "kct c_" + bit, "c_le" + n, col(bit), A.mult)
        ts(col("lx" + n), vec("i0"), 4.0, A.mult, "kct", "c_lx" + n)
        tt(col("lt" + n), col("lx" + n), col("le" + n), A.subtract, "c_lx%s c_le%s" % (n, n), "c_lt" + n)
        k = 2 * (int(n) - 1)
        act(T.ci1[:, k::4], om("w" + n), "w%s c_lt%s" % (n, n), "ci1_%d" % k, scale=col("lt" + n))
        act(T.ci1[:, k + 1::4], om("w" + n), "w%s c_le%s" % (n, n), "ci1_%d" % (k + 1), scale=col("le" + n))
    act(T.ci2[:, 0::4], om("w0"), "w0 c_lx1 ci2", "ci2_", scale=col("lx1"))
    quant("qci1", T.ci1[:], "ci1_0 ci1_1 ci1_2 ci1_3")
    quant("qci2", T.ci2[:], "ci2 ci2_")
    for c, w in (("cb", "w"), ("cbw", "u")):
        act(T[c][:, 0::4], om(w + "g"), "%s %sg kct" % (c, w), c + "_0", scale=vec("i0"))
        act(T[c][:, 1::4], om(w + "o"), "%s %so kct" % (c, w), c + "_1", scale=vec("i0"))
        quant("q" + c, T[c][:], "%s %s_0 %s_1" % (c, c, c))
    for k in range(3):
        r = 11 + k
        ts(T.cpw[:, 4 * r + 1 + k::64], T.rel0[:, r::16], vec("i0"), A.mult, "rel0 kct", "cpw", -2.0, A.mult)
    quant("qcpw", T.cpw[:], "cpw")
    act(T.ck[:, 0::4], T.rel0[:], "rel0 kct ck", "ck_", scale=vec("kv"))
    quant("qck", T.ck[:], "ck ck_")
    ts(T.ckg[:, 0::4], T.rel0[:], vec("i0"), A.mult, "rel0 kct", "ckg", 8.0, A.mult)
    quant("qckg", T.ckg[:], "ckg")
    ts(T.cn2[:, 0::4], T.rel0[:], vec("bb"), A.mult, "rel0 kct", "cn2")
    ts(T.cn2[:, 1::4], T.rel0[:], vec("bb"), A.mult, "rel0 kct", "cn2", 8.0, A.mult)
    quant("qcn2", T.cn2[:], "cn2")
    quant("qv", T.vt[:], "vt")
    for t in range(R):
        quant("aq%d" % t, T.zero[:, 0:512], "zero", k="aqz%d" % t, a=64, b=192)
    def routes_tables():
        ts(T.nat[:], T.inat[:], col("b3"), A.add, "inat c_b3", "nat")
        for k in range(3):
            sl = slice(20 * k, 20 * k + 20)
            tt(T.lwd[:, sl], T.lki[:, sl], T.nat[:], A.subtract, "lki nat", "lwd%d" % k)
            if k:
                ts(T.lwd[:, sl], T.lwd[:, sl], col("m%d" % k), A.add, "lwd%d c_m%d" % (k, k), "lwd%d" % k)
            fill(T.kcst[:, sl], (0, 1, 6)[k], "kcst")
            for a in range(4):
                s4 = slice(80 * k + 20 * a, 80 * k + 20 * a + 20)
                tt(T.lwd4[:, s4], T.lk4[:, 60 * a + 20 * k:60 * a + 20 * k + 20], T.nat[:], A.subtract, "lk4 nat", "lwd4%d%d" % (k, a))
                if k:
                    act(T.lwd4[:, s4], T.lwd4[:, s4], "lwd4%d%d" % (k, a), "lwd4%d%d" % (k, a), f=F.Identity, bias=640.0 * ((a ^ k) - a))
                ts(T.kc4[:, s4], T.kcst[:, sl], col("n%d" % a), A.add, "kcst c_n%d" % a, "kc4")
        for a in range(4):
            act(T.nat4[:, 20 * a:20 * a + 20], T.nat[:], "nat", "nat4", f=F.Identity, bias=640.0 * a)
        ts(T.nat[:], T.inat[:], col("oa"), A.add, "inat c_oa", "nat")

    LWD = "lwd0 lwd1 lwd2"
    LWD4 = " ".join("lwd4%d%d" % (k, a) for k in range(3) for a in range(4))

    def scan(n):
        op("v", "mk sc0", "sc", lambda e: e.tensor_tensor_scan(T.sc[:, 0:n], T.sc0[:, 0:n], T.mk[:, 0:n], 0.0, A.mult, A.add))

    def table(out, ok, src, reads, n=C):
        tt(T.mk[:, 0:n], src, T.mask[:, 0:n], A.mult, reads + " mask", "mk")
        scan(n)
        cp(out, T.sc[:, 15:n:16], "sc", ok)

    def spread4(dst, src, w, do=0, so=0, pitch=None):
        m = []
        for h in range(8):
            a = do + (pitch or w) * ((h & 1) + 2 * (h >> 2))
            for d in (h, h ^ 1, h ^ 4, h ^ 5):
                m.append(("y", dst[16 * d:16 * d + 16, a:a + w], src[16 * h:16 * h + 16, so:so + w]))
        return m

    def nsw(k):
        return T.ns[:, 320 * k:320 * k + 320]


    hold[0] = False
    for t in range(R):
        now, old = "%d" % (t % 2), "%d" % ((t + 1) % 2)
        if t:
            quant("qx", T.xt[:], "xt")
        for bank, la in ((5, 512), (6, 512), (4, 384), (1, 0), (2, 128), (3, 256)):
            mm(bank, "ua", "qx", True, True, la=la, lk="uac uas")
        op("v", "ps5", "tc", lambda e: e.transpose(T.tc[:], ps(5)))
        op("v", "ps4", "tb", lambda e: e.transpose(T.tb[:], ps(4)))
        tt(T.eqo[:], ps(5), T.tc[:], A.is_equal, "ps5 tc", "eqo")
        tt(T.eqe[:], ps(4), T.tb[:], A.is_equal, "ps4 tb", "eqe")
        for s, n in ((1, "eqo"),):
            for a in range(4):
                h = slice(32 * a, 32 * a + 32)
                asel(T.rt5[h, s::4], T[n][h, :], [[0, 10], [1, 32]], A.is_gt, 0, -1, n + " rt5", "rt5_%d%d" % (s, a))
        if t == 0:
            iota(T.iot[:], [[1, 2560]], 0, 0, "iot", True)
            iota(T.num[:], [[1280, 2], [320, 2], [1, 640]], 0, 0, "num", True)
            for k in range(3):
                act(nsw(k), ps(1 + k), "ps%d" % (1 + k), "ns%d" % k)
            act(T.srt[:], ps(1), "ps1", "srt")
            act(T.lrow[:], T.ioj[:].indirect(lks(0)), "ioj lk16", "lrow")
        def sign(b):
            so = 320 * (b % 3)
            act(T.sg[:, so:so + 320], ps(6), "ps6 tc", "sg%d" % (b % 3), f=F.Sign, scale=-1.0, bias=T.tc[:, 32 * b:32 * b + 1])

        sign(0)
        lastw["rt4_3x"] = []
        for b in range(9):
            e = 32 * b + 32
            sg, so = "sg%d" % (b % 3), 320 * (b % 3)
            if b < 8:
                sign(b + 1)
            n, s = "rt%d" % (b // 2), 2 + b % 2
            act(T[n][:, s:4 * e:4], T.sg[:, so:so + e], sg, "%s_%d" % (n, s), f=F.Sign, scale=-1.0, bias=-0.5)
            if e < C:
                act(T[n][:, 4 * e + s::4], T.sg[:, so + e:so + C], sg, "%s_%dx" % (n, s), f=F.Sign, scale=-1.0, bias=0.5)
            else:
                lastw["%s_%dx" % (n, s)] = []
        rk = 0

        def count(q, last=False):
            n = "rt%d" % q
            keys = " ".join("%s_%d" % (n, s) for s in range(4)) + " " + " ".join("%s_%dx" % (n, s) for s in range(4))
            if q == 5:
                keys = "rt5 rt5_0 " + " ".join("rt5_1%d" % a for a in range(4))
            d = ("ra_", "rb_")[q % 2]
            quant(d, T[n][:], keys)
            mm(7, "qcr5" if q == 5 else "qcr", d, q == 0, q == 5)

        for b in range(10):
            e = 32 * b + 32
            n, s = "rt%d" % (b // 2), b % 2
            p = T.tb[:, 32 * b:32 * b + 1]
            ts(T[n][:, s:4 * e:4], ps(4, 0, e), p, A.is_gt, "ps4 tb", "%s_%d" % (n, s))
            if e < C:
                ts(T[n][:, 4 * e + s::4], ps(4, e, C), p, A.is_ge, "ps4 tb", "%s_%dx" % (n, s))
            else:
                lastw["%s_%dx" % (n, s)] = []
            if b in (5, 7, 9):
                if t == 0 and b == 5:
                    ones()
                    quant("qcr", T.cr[:], "cr_0 cr_1 cr_2 cr_3")
                count(rk)
                rk += 1
        ts(T.rt4[:, 3::4], ps(5), T.tc[:, 288:289], A.is_gt, "ps5 tc", "rt4_3", 2.0, A.mult)
        if t == 0:
            quant("qcr5", T.cr5[:], "cr5 cr5_0 cr5_1")
            bits()
        tt(T.rt5[:, 0::4], T.eqe[:], T.tri[:], A.mult, "eqe tri rt5", "rt5_0")
        if t == 0:
            own = T.srt[:]
            for k in (1, 2):
                for s, f in ((0, A.is_lt), (1, A.is_le)):
                    i = 2 * (k - 1) + s
                    tt(T.flg[:, i::4], nsw(k).indirect(lks(k)), own, f, "srt ns%d lk16" % k, "flg%d" % i)
            quant("sq", T.flg[:], "flg0 flg1 flg2 flg3")
            tt(T.lrow[:], T.lrow[:], T.ioj[:], A.is_lt, "lrow ioj", "lrow")
            tt(T.g1[:], nsw(0).indirect(lks(0)), own, A.is_le, "srt ns0 lk16", "g1")
            tt(T.g2[:], nsw(0).indirect(lks(0)), own, A.is_lt, "srt ns0 lk16", "g2")
            tt(T.g1[:], T.g1[:], T.lrow[:], A.min, "g1 lrow", "g1")
            tt(T.kt[:, 0::4], T.g1[:], T.g2[:], A.max, "g1 g2 kt", "kt_0")
            quant("kq", T.kt[:], "kt kt_0")
            tt(T.gp[:, 1::4], T.tb[:], T.tb[:], A.is_equal, "tb gp", "gp_1")
        def unpack(b):
            bank = (4, 5, 6, 4)[b]
            mm(bank, "eb", "qx", True, True, la=128 * b)
            act(T.fo[:, 320 * b:320 * b + 320], ps(bank), "ps%d" % bank, "fo%d" % b)
            if b % 2:
                dma(spread4(T.f4, T.fo, 640, do=1280 * (b - 1), so=320 * (b - 1)), "fd%d" % t, "fo%d fo%d" % (b - 1, b), "f4%d" % (b // 2))

        late = []
        for q in (3, 4, 5):
            count(q)
        if t:
            for b in range(3):
                unpack(b)
            late.append(unpack)
            for k in (2, 1, 0):
                act(nsw(k), ps(1 + k), "ps%d" % (1 + k), "ns%d" % k)
        if t == 0:
            flush()
            mm(0, "qci1", "sq", True, False)
            mm(0, "qci2", "kq", False, False)
        ts(T.gp[:, 0::4], ps(7), col("t63"), A.is_lt, "ps7 c_t63 gp", "gp_0")
        quant("gq" + now, T.gp[:], "gp gp_0 gp_1")
        if t:
            mm(0, "qcs", "kq", True, False)
        mm(0, "qcb", "gq" + now, False, True)
        for fn in late:
            fn(3)
        ex = {i: [] for i in range(6)}

        def later(i):
            def put(fn):
                ex[i].append(fn)
            return put

        @later(0)
        def _():
            scan(C)
            ts(T.sl[:], ps(7), col("s1"), A.add, "ps7 c_s1 c_s2", "sl", col("s2"), A.min)
            dma(spread4(T.ds4, T.sl, 320, do=320, pitch=640), "dd%d" % t, "sl", "ds4s")
            if t == 0:
                unpack(0)
                unpack(1)
            else:
                act(T.g2[:], nsw(2).indirect(lks(2)), "ns2 lk16", "g2")

        tt(T.mk[:], ps(7), T.mask[:], A.mult, "ps7 mask", "mk")

        def ready():
            ts(u("rw"), T.sc[:, 15:C:16], col("off"), A.add, "sc c_off", "rw")

        @later(1)
        def _():
            op("v", "rw ioj", "srt", lambda e: e.tensor_copy(T.srt[:].indirect(u("rw")), T.ioj[:]))
            if t == 0:
                unpack(2)
                unpack(3)
                act(T.g2[:], nsw(2).indirect(lks(2)), "ns2 lk16", "g2")
            else:
                act(T.g1[:], nsw(1).indirect(lks(1)), "ns1 lk16", "g1")

        @later(2)
        def _():
            tt(T.mk[:, 0:64], T.srt[:, 0:64], T.mask[:, 0:64], A.mult, "srt mask", "mk")
            tt(T.pp[:, 2::4], nsw(0).indirect(lks(0)), T.g2[:], A.is_le, "ns0 lk16 g2 pp", "pp2")
            scan(64)
            cp(u("lg"), T.sc[:, 15:64:16], "sc", "lg")
            for b in range(4):
                act(T.et[:, b:256:4], T.fo[:, 320 * b:320 * b + 320].indirect(u("lg")), "lg et fo%d" % b, "et_%d" % b, scale=2.0)
            if t == 0:
                act(T.g1[:], nsw(1).indirect(lks(1)), "ns1 lk16", "g1")

        @later(3)
        def _():
            quant("qe%d" % t, T.et[:], "et et_0 et_1 et_2 et_3")
            settle("g", lastw["qe%d" % t])
            rid, pid, _ = topo.addr(nxt)
            m = topo.mask(core, nxt)
            ne = len(topo.engines(core, nxt))
            for d, s, bc in (("aq%dc" % t, "qec", True), ("aq%ds" % t, "qes", False)):
                o, i = T[d][:, 0:64], T[s][:, 128 * t:128 * t + 64]
                if bc:
                    o, i = o.bitcast(dt.uint8), i.bitcast(dt.uint8)
                g.remote_dma(o, i, T.sem["arr%d" % t], T.sem["snt%d" % t], pid, rid, m)
            tot["arr%d" % t] = 2 * ne
            tot["snt%d" % t] = 2 * ne
            lastw["aq%d" % t] = [("arr%d" % t, 2 * ne, {}, "dma")]
            tt(T.pp[:, 3::4], nsw(1).indirect(lks(1)), T.g2[:], A.is_le, "ns1 lk16 g2 pp", "pp3")

        @later(2)
        def _():
            if t == 0:
                routes_tables()

        @later(4)
        def _():
            tt(T.pp[:, 1::4], nsw(0).indirect(lks(0)), T.g1[:], A.is_le, "ns0 lk16 g1 pp", "pp1")
            quant("pq" + now, T.pp[:], "pp pp1 pp2 pp3")

        def layer():
            for b in range(4):
                mm(1 + b, "qw", "aq%d" % t, True, True, la=128 * b, n=128, rk="aq%d aqz%d" % (t, t))
            for b in range(4):
                act(T.ho[:, 80 * b:80 * b + 64], ps(1 + b, 0, 64), "ho ps%d" % (1 + b), "ho_%d" % b, scale=0.015625)
            dma(spread4(T.h4, T.ho, 320), "hd%d" % t, "ho ho_0 ho_1 ho_2 ho_3", "h4")

        for i in range(SWEEPS):
            ts(T.pub[:], ps(0), vec("lo"), A.max, "ps0 kct", "pub", vec("hi"), A.min)
            mm(0, "qcb", "gq" + now, True, False)
            if i == 1:
                ready()
            act(T.st[:, 0::4], T.pub[:].indirect(lks(0)), "st pub lk16", "st_0")
            cp(T.st[:, 1::4], T.pub[:].indirect(lks(1)), "st pub lk16", "st_1")
            act(T.st[:, 3::4], T.pub[:], "st pub", "st_3")
            cp(T.st[:, 2:64 * SPLIT:4], T.pub[:].indirect(lks(2, 0, SPLIT)), "st pub lk16", "st_2")
            act(T.st[:, 64 * SPLIT + 2::4], T.pub[:].indirect(lks(2, SPLIT, 20)), "st pub lk16", "st_2x")
            if i == SWEEPS - 1:
                mm(5, "qcbw", "gq" + now, True, False)
                mm(5, "qcpw", "pq" + now, False, False)
            quant("sq", T.st[:], "st st_0 st_1 st_2 st_2x st_3")
            if i == SWEEPS - 1:
                mm(5, "qcmw", "sq", False, True)
                mm(6, "qckg", "gq" + now, True, False)
            mm(0, "qcm", "sq", False, True)
            for fn in ex[i]:
                fn()
        act(T.kt[:, 1::4], ps(0), "ps0 kt", "kt_1")
        ts(T.kt[:, 0::4], ps(5), 0.0, A.max, "ps5 kt", "kt_0", 1.0, A.min)
        quant("kq", T.kt[:], "kt kt_0 kt_1")
        mm(6, "qck", "kq", False, True)
        table(T.ki4[:, 0:20], "ki0", ps(6), "ps6")
        for a in range(1, 4):
            cp(T.ki4[:, 20 * a:20 * a + 20], T.sc[:, 15:C:16], "sc", "ki%d" % a)
        for k in range(3):
            op("v", "ki0 ki1 ki2 ki3", "kb%d" % k, lambda e: e.tensor_scalar(T.kb4[:, 80 * k:80 * k + 80], T.ki4[:], (11, 13, 14)[k], None, A.bitwise_and))
        tt(T.zt[:, 0::4], T.kb4[:], T.kc4[:], A.is_equal, "kb0 kb1 kb2 kc4 zt", "zt_")
        quant("zq", T.zt[:], "zt zt_")
        mm(5, "qcz", "zq", True, True, n=240)
        for k in range(3):
            tt(T.kz[:, 20 * k:20 * k + 20], T.kb4[:, 80 * k:80 * k + 20], T.kcst[:, 20 * k:20 * k + 20], A.is_equal, "kb%d kcst" % k, "kz%d" % k)
        tt(T.kd[:], T.kz[:], T.lwd[:], A.mult, "kz0 kz1 kz2 " + LWD, "kd")
        tt(T.kd4[:], ps(5, 0, 240), T.lwd4[:], A.mult, "ps5 " + LWD4, "kd4")
        tt(T.dl[:], T.kd[:, 0:20], T.nat[:], A.add, "kd nat", "dl")
        tt(T.kd4[:, 0:80], T.kd4[:, 0:80], T.nat4[:], A.add, "kd4 nat4", "kd4a")
        tt(T.kd4[:, 80:160], T.kd4[:, 80:160], T.kd4[:, 160:240], A.add, "kd4", "kd4b")
        tt(T.dl[:], T.dl[:], T.kd[:, 20:40], A.add, "dl kd", "dl")
        tt(T.kd4[:, 0:80], T.kd4[:, 0:80], T.kd4[:, 80:160], A.add, "kd4a kd4b", "kd4c")
        tt(T.dl[:], T.dl[:], T.kd[:, 40:60], A.add, "dl kd", "dl")
        cp(u("dl4"), T.kd4[:, 0:80], "kd4c", "dl4")
        cp(u("dl16"), T.dl[:], "dl", "dl16")
        lastw["kd4"] = lastw["kd4c"]
        readers["kd4"] = list(readers.get("kd4c", []))
        for a in (0, 1):
            act(T.ds4[:, 640 * a:640 * a + 320], T.iot[:].indirect(u("dl4", 20 * a, 20 * a + 20)), "dl4 iot", "ds4%d" % a)
        for a in (2, 3):
            cp(T.ds4[:, 640 * a:640 * a + 320], T.iot[:].indirect(u("dl4", 20 * a, 20 * a + 20)), "dl4 iot", "ds4%d" % a)
        DS = "ds40 ds41 ds42 ds43 ds4s "

        def fwin(b):
            o = 2560 * (b // 2) + 320 * (b % 2)
            return T.f4[:, o:o + 2240]

        for b in range(4):
            act(T.zd[:, 320 * b:320 * b + 320], fwin(b).indirect(u("dl16")), "dl16 f4%d" % (b // 2), "zd%d" % b)
            if b == 0:
                layer()
        cur = "dl16"
        for n in ("c1", "c2", "e16"):
            table(u(n), n, T.ds4[:, 0:2240].indirect(u(cur)), DS + cur)
            cur = n
        if t == R - 1:
            act(T.lrow[:], T.num[:].indirect(u("e16")), "num e16", "lrow")
            act(T.ndr[:, 0:320], T.lrow[:], "lrow c_cl", "ndr_0", f=F.Identity, bias=col("cl"))
        tt(T.mk[:], T.ds4[:, 320:2560].indirect(u("e16")), T.mask[:], A.mult, DS + "e16 mask", "mk")
        for b in range(4):
            if b == 1:
                op("v", "mk sc0", "sc", lambda e: e.tensor_tensor_scan(T.sc[:], T.sc0[:], T.mk[:], 0.0, A.mult, A.add))
            if b == 2:
                cp(u("hl"), T.sc[:, 15:C:16], "sc", "hl")
            tt(T.zz[:, 320 * b:320 * b + 320], fwin(b).indirect(u("e16")), T.zd[:, 320 * b:320 * b + 320], A.add, "e16 zd%d f4%d" % (b, b // 2), "zz%d" % b)
        for b in range(4):
            tt(T.xt[:, b::4], T.h4[:, 80 * b:80 * b + 1040].indirect(u("hl")), T.zz[:, 320 * b:320 * b + 320], A.add, "hl h4 zz%d" % b, "xt%d" % b)

    quant("qx", T.xt[:], "xt")
    mm(1, "qv", "qx", True, True)
    dma([("y", T.oc[:], T.qxc[:].bitcast(dt.uint8))] + [("y", T.osc[4 * k:4 * k + 4, :], T.qxs[32 * k:32 * k + 4, :]) for k in range(4)], "oco", "qx", "oc_")
    act(T.ysb[:], ps(1), "ps1", "ysb")
    dma([("s", T.y[:], T.ysb[:])], "yo", "ysb", "y_")
    ts(T.flg[:, 0::4], ps(0), 3.5, A.is_ge, "ps0", "flg")
    ts(T.flg[:, 1::4], ps(0), 1.0, A.is_equal, "ps0", "flg")
    quant("kq", T.flg[:], "flg")
    mm(7, "qcn2", "kq", True, True)
    cp(T.ndr[:, 320:640], ps(7), "ps7", "ndr_1")
    dma([("y", T.nd[:, :], T.ndr[0:128:16, :])], "ndo", "ndr_0 ndr_1", "nd_")
    for sem in sorted(tot):
        if know["g"].get(sem, 0) < tot[sem]:
            g.wait_ge(T.sem[sem], tot[sem])
